import numpy as np
import ml_dtypes


def mxq(x, axis, fmt="e4m3"):
    dtype, down = {"e4m3": (ml_dtypes.float8_e4m3fn, 7), "e5m2": (ml_dtypes.float8_e5m2, 14)}[fmt]
    v = np.moveaxis(np.asarray(x, np.float32).astype(ml_dtypes.bfloat16).astype(np.float64), axis, -1)
    blocks = v.reshape(v.shape[:-1] + (-1, 32))
    amax = np.abs(blocks).max(-1, keepdims=True)
    byte = np.maximum(np.where(amax > 0, np.frexp(amax)[1] - 1 + 127, 0) - down, 1)
    scale = np.exp2(byte - 127.0)
    codes = (blocks / scale).astype(np.float32).astype(dtype).astype(np.float64)
    return np.moveaxis((codes * scale).reshape(v.shape), -1, axis)


WIDE = False


def mx_kscale(k):
    if not WIDE:
        return np.ones(k)
    levels = np.array([10, -10, 5, -5, 0])
    if k % 512:
        return np.exp2(np.random.permutation(np.resize(levels, k // 32))).repeat(32)
    a = np.empty((k // 512, 16))
    for p in range(k // 512):
        a[p, :8] = np.random.permutation(np.resize(levels, 8))
        for g in range(8):
            far = levels[np.abs(levels - a[p, g]) >= 10]
            a[p, g + 8] = far[np.random.randint(len(far))]
    return np.exp2(a.ravel()).repeat(32)


BF16 = ml_dtypes.bfloat16


def bf(x):
    return np.asarray(x, np.float32).astype(BF16)


def f64(x):
    return np.asarray(x).astype(np.float64)


E2M1 = np.array([0.0, 0.5, 1.0, 1.5, 2.0, 3.0, 4.0, 6.0, -0.0, -0.5, -1.0, -1.5, -2.0, -3.0, -4.0, -6.0])


def pack_weight(w, fmt):
    k, n = w.shape
    w = f64(bf(w)).reshape(k // 32, 32, n)
    amax = np.abs(w).max(1)
    if fmt == "e4m3":
        byte = np.frexp(amax)[1] - 1 + 127 - 7
    else:
        mant, ex = np.frexp(amax / 6.0)
        byte = np.where(mant > 0.5, ex, ex - 1) + 127
    byte = np.clip(np.where(amax > 0, byte, 1), 1, 254)
    scaled = (w * np.exp2(127.0 - byte)[:, None, :]).reshape(k, n).astype(np.float32)
    by_word = np.ascontiguousarray(scaled.reshape(k // 512, 128, 4, n).transpose(0, 1, 3, 2))
    if fmt == "e4m3":
        words = by_word.astype(ml_dtypes.float8_e4m3fn).view(np.uint8)
    else:
        c = by_word.astype(ml_dtypes.float4_e2m1fn).view(np.uint8) & 0xF
        words = c[..., 0::2] | (c[..., 1::2] << 4)
    return np.ascontiguousarray(words), np.ascontiguousarray(byte.astype(np.uint8).reshape(k // 512, 16, n))


def unpack_weight(words, scales, fmt):
    g, p, n, _ = words.shape
    if fmt == "e4m3":
        vals = np.ascontiguousarray(words).view(ml_dtypes.float8_e4m3fn).astype(np.float64)
    else:
        nib = np.empty((g, p, n, 4), np.uint8)
        nib[..., 0::2] = words & 0xF
        nib[..., 1::2] = words >> 4
        vals = E2M1[nib]
    vals = vals * np.repeat(np.exp2(scales.astype(np.float64) - 127.0), 8, axis=1)[..., None]
    return vals.transpose(0, 1, 3, 2).reshape(g * 512, n)

E4M3FN = np.array([(-1.0 if i & 128 else 1.0) * ((1.0 + (i & 7) / 8.0) * 2.0 ** (((i >> 3) & 15) - 7) if i & 120 else (i & 7) * 2.0 ** -9) for i in range(256)])


def e4m3fn_bytes(y):
    return np.clip(np.asarray(y, np.float64), -448.0, 448.0).astype(np.float32).astype(ml_dtypes.float8_e4m3fn).view(np.uint8)


def e4m3fn_values(b):
    return E4M3FN[b]


B, L, D, E = 256, 4, 512, 1024


def erf(a):
    c = np.clip(a, -6.0, 6.0)
    c2 = c * c
    term = c
    total = c
    for n in range(1, 150):
        term = term * (2.0 * c2 / (2.0 * n + 1.0))
        total = total + term
    v = 2.0 / np.sqrt(np.pi) * np.exp(-c2) * total
    return np.where(np.abs(a) <= 6.0, v, np.sign(a))


def gelu_erf(v):
    return 0.5 * v * (1.0 + erf(v / np.sqrt(2.0)))


def softplus(r):
    return np.maximum(r, 0.0) + np.log(1.0 + np.exp(-np.abs(r)))


def draw0():
    s1, s2 = mx_kscale(D), mx_kscale(D)
    t = mx_kscale(E)
    c = 1.0 / np.sqrt(D)
    x = bf(np.random.standard_normal((B, L, D)) * s1)
    y = bf(np.random.standard_normal((B, D)) * s2)
    wu_words, wu_scales = pack_weight(np.random.standard_normal((D, E)) * c / s1[:, None] * t[None, :], "e4m3")
    bu = bf(np.random.standard_normal(E) * 0.3 * t)
    wg_words, wg_scales = pack_weight(np.random.standard_normal((D, E)) * c / s2[:, None], "e4m3")
    bg = bf(np.random.standard_normal(E) * 0.3)
    gain = bf((1.0 + 0.1 * np.random.standard_normal(E)) / t)
    return {
        "x": x,
        "y": y,
        "wu_words": wu_words,
        "wu_scales": wu_scales,
        "bu": bu,
        "wg_words": wg_words,
        "wg_scales": wg_scales,
        "bg": bg,
        "gain": gain,
    }


def core(x, y, wu_words, wu_scales, bu, wg_words, wg_scales, bg, gain):
    n, patches, _ = x.shape
    u = (mxq(f64(x), 2, "e4m3") @ unpack_weight(wu_words, wu_scales, "e4m3")) + f64(bu)
    g = f64(gain) * gelu_erf((mxq(f64(y), 1, "e4m3") @ unpack_weight(wg_words, wg_scales, "e4m3")) + f64(bg))
    u_flat = u.reshape(n * patches, u.shape[-1])
    s = (mxq(g, 1, "e4m3") @ mxq(u_flat, 1, "e4m3").T) / 16.0
    s = s.reshape(n, n, patches)
    idx = np.arange(n)
    positive = (idx[:, None] == idx[None, :])[:, :, None]
    r = np.where(positive, -s, s)
    return softplus(r)


def setup_inputs():
    drawn = draw0()
    full = np.asarray(drawn['x']).astype(np.float64)
    scale = (np.abs(full).reshape(256, 4, 4, 128).max(axis=(3,)) / 448.0).astype(np.float32)
    given = {}
    for key, value in drawn.items():
        if key == 'x':
            given['x_bytes'] = e4m3fn_bytes(full / np.repeat(scale.astype(np.float64), 128, axis=2))
            given['x_scale'] = scale
        else:
            given[key] = value
    return given


def reference(x_bytes, x_scale, y, wu_words, wu_scales, bu, wg_words, wg_scales, bg, gain):
    return core(e4m3fn_values(x_bytes) * np.repeat(x_scale.astype(np.float64), 128, axis=2), y, wu_words, wu_scales, bu, wg_words, wg_scales, bg, gain)

@@ -1,0 +1,481 @@
+from contextlib import ExitStack
+
+import concourse.mybir as mybir
+from concourse.masks import make_identity
+
+F32 = mybir.dt.float32
+BF16 = mybir.dt.bfloat16
+I32 = mybir.dt.int32
+U32 = mybir.dt.uint32
+U8 = mybir.dt.uint8
+FP8 = mybir.dt.float8_e4m3fn
+FP8X4 = mybir.dt.float8_e4m3fn_x4
+ACT = mybir.ActivationFunctionType
+ALU = mybir.AluOpType
+
+B, L, D, E = 256, 4, 512, 1024
+P = 128
+GROUPS = 4
+TOK = 256
+FLOPS = 2 * (B * L * D * E + B * D * E + B * E * B * L)
+
+
+def tile_deepinfomaxlocalglobaljsdmap_d1p_kernel(
+    tc, x_bytes, x_scale, y, wu_words, wu_scales, bu, wg_words, wg_scales, bg, gain, out
+):
+    nc = tc.nc
+    with ExitStack() as ctx:
+        sb = ctx.enter_context(tc.tile_pool(name="sb", bufs=1))
+        ps = ctx.enter_context(tc.psum_pool(name="ps", bufs=1))
+        ctx.enter_context(tc.manual_schedule())
+
+        def keep(name, shape, dtype):
+            return sb.tile(shape, dtype, name=name, align_bytes=64)
+
+        def bank(k):
+            return ps.tile([P, 512], F32, name="bank%d" % k)
+
+        x_rows = x_bytes.rearrange("b l k -> (b l) k").rearrange("(h p c) k -> p h (c k)", p=P, c=2)
+        xs_rows = x_scale.rearrange("b l q -> (b l) q").rearrange("(h p c) q -> p h (c q)", p=P, c=2)
+        out_rows = out.rearrange("(a p) j l -> p a (j l)", p=P)
+
+        xs = keep("xs", [P, GROUPS, 8], F32)
+        xb0 = keep("xb0", [P, 1, 2 * D], U8)
+        xb1 = keep("xb1", [P, 1, 2 * D], U8)
+        xb23 = keep("xb23", [P, 2, 2 * D], U8)
+        xb = [xb0[:, 0, :], xb1[:, 0, :], xb23[:, 0, :], xb23[:, 1, :]]
+        xw = [[keep("xw%d_%d" % (h, c), [P, D], BF16) for c in range(2)] for h in range(GROUPS)]
+        yb = keep("yb", [P, 2, D], BF16)
+        xt = [keep("xt%d" % h, [P, 4 * TOK], BF16) for h in range(GROUPS + 1)]
+        xq = [keep("xq%d" % h, [P, TOK], U32) for h in range(GROUPS + 1)]
+        xqs = [keep("xqs%d" % h, [P, TOK], U8) for h in range(GROUPS + 1)]
+        w_raw = {w: keep("wraw_%s" % w, [P, E], U32) for w in "ug"}
+        w_perm = {(w, g): keep("wperm_%s%d" % (w, g), [P, 512], U32) for w in "ug" for g in range(2)}
+        s_raw = {w: keep("sraw_%s" % w, [P, E], U8) for w in "ug"}
+        s_perm = {w: keep("sperm_%s" % w, [P, E], U8) for w in "ug"}
+        vec_rows = {w: keep("vec_rows_%s" % w, [P, 256], BF16) for w in "ug"}
+        vec = {w: keep("vec_%s" % w, [P, 2, 8], F32) for w in "ug"}
+        ident = keep("ident", [P, P], F32)
+        ident_bf = keep("ident_bf", [P, 8], BF16)
+        half = keep("half", [P, 1], F32)
+        warm = keep("warm", [P, 1], F32)
+        sign = keep("sign", [P, 4, 64], F32)
+        ub = [[keep("ub%d_%d" % (h, g), [P, 4 * TOK], BF16) for g in range(2)] for h in range(GROUPS)]
+        uq = [[keep("uq%d_%d" % (h, g), [P, TOK], U32) for g in range(2)] for h in range(GROUPS)]
+        uqs = [[keep("uqs%d_%d" % (h, g), [P, TOK], U8) for g in range(2)] for h in range(GROUPS)]
+        gl = [keep("gl%d" % g, [P, 4, B], F32) for g in range(2)]
+        gb = [keep("gb%d" % g, [P, 4 * B], BF16) for g in range(2)]
+        gq = [keep("gq%d" % g, [P, B], U32) for g in range(2)]
+        gqs = [keep("gqs%d" % g, [P, B], U8) for g in range(2)]
+        PIECES = ((0, 0, 256), (1, 0, 256), (2, 0, 256), (3, 0, 128), (3, 128, 128))
+        th = {(h, lo): keep("th%d_%d" % (h, lo), [P, 2, n], F32) for h, lo, n in PIECES}
+        lg = {(h, lo): keep("lg%d_%d" % (h, lo), [P, 2, n], F32) for h, lo, n in PIECES}
+        r = {(h, lo): keep("r%d_%d" % (h, lo), [P, 2, n], F32) for h, lo, n in PIECES}
+        res = {(h, lo): keep("res%d_%d" % (h, lo), [P, 2, n], F32) for h, lo, n in PIECES}
+
+        flat = {("u", h, g): keep("flat_u%d_%d" % (h, g), [P, 4, TOK], BF16) for h in range(GROUPS) for g in range(2)}
+        flat.update({("g", g): keep("flat_g%d" % g, [P, 4, B], BF16) for g in range(2)})
+
+        words_in = {"u": wu_words, "g": wg_words}
+        scales_in = {"u": wu_scales, "g": wg_scales}
+        held = {}
+
+        def load_scales(w):
+            for q in range(4):
+                nc.sync.dma_start(
+                    out=s_raw[w][32 * q : 32 * q + 4, :].bitcast(I32),
+                    in_=scales_in[w][0, 4 * q : 4 * q + 4, :].bitcast(I32),
+                )
+
+        def words(w):
+            return words_in[w][0].rearrange("p n t -> p (n t)").bitcast(I32)
+
+        def widen(h, c, q, eng):
+            src = xb[h][:, c * D + 128 * q : c * D + 128 * (q + 1)].bitcast(FP8)
+            dst = xw[h][c][:, 128 * q : 128 * (q + 1)]
+            col = xs[:, h, 4 * c + q : 4 * c + q + 1]
+            if eng == "v":
+                nc.vector.tensor_scalar(out=dst, in0=src, scalar1=col, scalar2=None, op0=ALU.mult)
+            else:
+                nc.scalar.activation(out=dst, in_=src, func=ACT.Copy, scale=col)
+
+        def turn(h, k):
+            rows = [xw[h][c][:] for c in range(2)] if h < GROUPS else [yb[:, c, :] for c in range(2)]
+            t = bank(k)
+            held["t", h] = t
+            for c in range(2):
+                w32 = rows[c].bitcast(F32)
+                for u in range(2):
+                    j = 2 * c + u
+                    nc.tensor.transpose(t[:, 128 * j : 128 * (j + 1)], w32[:, u:256:2], ident[:])
+
+        def turn_out(h):
+            nc.scalar.copy(
+                out=xt[h][:].bitcast(F32).rearrange("k (p j) -> k p j", j=4),
+                in_=held["t", h][:].rearrange("k (j p) -> k p j", j=4),
+            )
+
+        def quant(codes, scales, src):
+            nc.vector.quantize_mx(out=codes[:].bitcast(FP8X4), scales=scales[:], in_=src[:])
+
+        def perm_words(w, g, eng):
+            src = w_raw[w][:, 512 * g : 512 * (g + 1)]
+            eng.tensor_copy(
+                out=w_perm[w, g][:].bitcast(I32).rearrange("p (t q r) -> p t q r", t=4, r=8),
+                in_=src.bitcast(I32).rearrange("p (q t r) -> p t q r", t=4, r=8),
+            )
+
+        def perm_scales(w, eng):
+            eng.tensor_copy(
+                out=s_perm[w][:].bitcast(I32).rearrange("p (t m r) -> p t m r", t=4, r=2),
+                in_=s_raw[w][:].bitcast(I32).rearrange("p (m t r) -> p t m r", t=4, r=2),
+            )
+
+        def first_mm(dst, w, g, t, h, cols):
+            nc.tensor.matmul_mx(
+                out=dst,
+                lhsT=w_perm[w, g][:, 128 * t : 128 * (t + 1)].bitcast(FP8X4),
+                lhsT_scale=s_perm[w][:, 256 * t + 128 * g : 256 * t + 128 * (g + 1)],
+                rhs=xq[h][:, cols].bitcast(FP8X4),
+                rhs_scale=xqs[h][:, cols],
+                start=True,
+                stop=True,
+            )
+
+        def u_mm(h, g, a, k):
+            t = bank(k)
+            held["u", h, g, a] = t
+            for j in range(4):
+                first_mm(t[:, 128 * j : 128 * (j + 1)], "u", g, j, h, slice(128 * a, 128 * (a + 1)))
+
+        def u_out(h, g, a):
+            nc.vector.tensor_tensor(
+                out=ub[h][g][:, 512 * a : 512 * (a + 1)].rearrange("p (n t) -> p n t", t=4),
+                in0=held["u", h, g, a][:].rearrange("p (t n) -> p n t", t=4),
+                in1=vec["u"][:, g, 0:4].unsqueeze(1).to_broadcast([P, 128, 4]),
+                op=ALU.add,
+            )
+
+        def u_quant(h, g, lo=0, n=TOK):
+            quant(uq[h][g][:, lo : lo + n], uqs[h][g][:, lo : lo + n], ub[h][g][:, 4 * lo : 4 * (lo + n)])
+
+        def u_mm_wide(h, g, a, k):
+            t = bank(k)
+            held["u", h, g, a] = t
+            for j in range(2):
+                first_mm(t[:, 256 * j : 256 * (j + 1)], "u", g, 2 * a + j, h, slice(0, TOK))
+
+        def u_bias(h, g, a):
+            for j in range(2):
+                t = 2 * a + j
+                nc.scalar.activation(
+                    out=flat["u", h, g][:, t, :],
+                    in_=held["u", h, g, a][:, 256 * j : 256 * (j + 1)],
+                    func=ACT.Identity,
+                    bias=vec["u"][:, g, t : t + 1],
+                )
+
+        def weave(dst, src):
+            nc.vector.tensor_copy(out=dst[:].rearrange("p (n t) -> p n t", t=4), in_=src[:].rearrange("p t n -> p n t"))
+
+        def u_weave(h, g):
+            weave(ub[h][g], flat["u", h, g])
+
+        def g_scale(g, a):
+            for j in range(2):
+                t = 2 * a + j
+                nc.scalar.activation(
+                    out=flat["g", g][:, t, :], in_=gl[g][:, t, :], func=ACT.Copy, scale=vec["g"][:, g, 4 + t : 5 + t]
+                )
+
+        def g_weave(g):
+            weave(gb[g], flat["g", g])
+
+        def g_mm(g, a, k):
+            t = bank(k)
+            held["g", g, a] = t
+            for j in range(2):
+                first_mm(t[:, 256 * j : 256 * (j + 1)], "g", g, 2 * a + j, GROUPS, slice(0, B))
+
+        def gelu(g, a):
+            for j in range(2):
+                t = 2 * a + j
+                nc.scalar.activation(
+                    out=gl[g][:, t, :],
+                    in_=held["g", g, a][:, 256 * j : 256 * (j + 1)],
+                    func=ACT.Gelu,
+                    bias=vec["g"][:, g, t : t + 1],
+                )
+
+        def g_gain(g, eng):
+            eng.tensor_tensor(
+                out=gb[g][:].rearrange("p (n t) -> p n t", t=4),
+                in0=gl[g][:].rearrange("p t n -> p n t"),
+                in1=vec["g"][:, g, 4:8].unsqueeze(1).to_broadcast([P, B, 4]),
+                op=ALU.mult,
+            )
+
+        def load_words(w, lo, n):
+            nc.sync.dma_start(out=w_raw[w][:, lo : lo + n].bitcast(I32), in_=words(w)[:, lo : lo + n])
+
+        def load_vec(w, v, src, eng):
+            eng.dma_start(
+                out=vec_rows[w][4 * v : 4 * v + 4, :].rearrange("t (m r) -> t m r", r=8),
+                in_=src.rearrange("(m t r) -> t m r", t=4, r=8),
+            )
+
+        def vec_mm(w, k):
+            t = bank(k)
+            held["v", w] = t
+            for g in range(2):
+                nc.tensor.matmul(
+                    t[:, 8 * g : 8 * (g + 1)], lhsT=vec_rows[w][:, 128 * g : 128 * (g + 1)], rhs=ident_bf[:],
+                    start=True, stop=True,
+                )
+
+        def vec_out(w):
+            nc.scalar.copy(out=vec[w][:].rearrange("p g v -> p (g v)"), in_=held["v", w][:, 0:16])
+
+        def warm_pe(k, n):
+            t = bank(k)
+            for j in range(n):
+                nc.tensor.matmul(t[:, 0:P], lhsT=ident[:], rhs=ident[:], start=True, stop=True)
+
+        def s_mm(h, k, lo=0, n=TOK):
+            t = bank(k)
+            held["s", h, lo] = t
+            for a in range(2):
+                for g in range(2):
+                    nc.tensor.matmul_mx(
+                        out=t[:, n * a : n * (a + 1)],
+                        lhsT=gq[g][:, 128 * a : 128 * (a + 1)].bitcast(FP8X4),
+                        lhsT_scale=gqs[g][:, 128 * a : 128 * (a + 1)],
+                        rhs=uq[h][g][:, lo : lo + n].bitcast(FP8X4),
+                        rhs_scale=uqs[h][g][:, lo : lo + n],
+                        start=(g == 0),
+                        stop=(g == 1),
+                    )
+
+        def s_abs(h, lo=0, n=TOK):
+            src = held["s", h, lo][:, 0 : 2 * n].rearrange("p (a n) -> p a n", a=2)
+            nc.scalar.activation(out=th[h, lo][:], in_=src, func=ACT.Abs, scale=1.0 / 32.0)
+
+        def s_tanh(h, lo=0, n=TOK):
+            nc.scalar.activation(out=th[h, lo][:], in_=th[h, lo][:], func=ACT.Tanh)
+
+        def s_sign(h, lo=0, n=TOK):
+            pick = [sign[:, 1:4:2, :], sign[:, 2:4, :], sign[:, 0:2, :], sign[:, 0:3:2, :]][h]
+            nc.vector.tensor_tensor(
+                out=r[h, lo][:].rearrange("p a (j l) -> p a j l", l=L),
+                in0=held["s", h, lo][:, 0 : 2 * n].rearrange("p (a j l) -> p a j l", a=2, l=L),
+                in1=pick[:, :, lo // L : (lo + n) // L].unsqueeze(3).to_broadcast([P, 2, n // L, L]),
+                op=ALU.mult,
+            )
+
+        def s_log(h, lo=0, n=TOK):
+            nc.scalar.activation(out=lg[h, lo][:], in_=th[h, lo][:], func=ACT.Ln, scale=0.5, bias=half[:])
+
+        def s_finish(h, lo=0, n=TOK):
+            nc.vector.scalar_tensor_tensor(
+                out=res[h, lo][:], in0=r[h, lo][:], scalar=0.0, in1=lg[h, lo][:],
+                op0=ALU.max, op1=ALU.subtract,
+            )
+
+        def s_store(h, lo, n):
+            nc.sync.dma_start(out=out_rows[:, :, TOK * h + lo : TOK * h + lo + n], in_=res[h, lo][:])
+
+        def x_quant(h):
+            quant(xq[h], xqs[h], xt[h])
+
+        def g_quant(g):
+            quant(gq[g], gqs[g], gb[g])
+
+        def make_sign():
+            nc.gpsimd.memset(sign[:], 1.0 / 16.0)
+            diag = sign[:].rearrange("p a j -> p (a j)")[:, 64:192]
+            nc.gpsimd.affine_select(
+                out=diag, in_=diag, pattern=[[-1, P]], compare_op=ALU.not_equal, fill=-1.0 / 16.0, base=0,
+                channel_multiplier=1,
+            )
+
+        def load_x(tile, lo, n):
+            nc.sync.dma_start(out=tile[:], in_=x_rows[:, lo : lo + n, :])
+
+        def load_y():
+            nc.sync.dma_start(out=yb[:].rearrange("p c k -> p (c k)"), in_=y.rearrange("(p c) k -> p (c k)", c=2))
+
+        nc.vector.memset(vec_rows["g"][:], 0.0)
+        make_identity(nc, ident[:])
+        nc.vector.tensor_copy(out=ident_bf[:], in_=ident[:, 0:8])
+        nc.vector.memset(half[:], 0.5)
+        nc.sync.dma_start(out=xs[:], in_=xs_rows)
+        load_x(xb0, 0, 1)
+        nc.scalar.activation(out=warm[:], in_=half[:], func=ACT.Gelu)
+        widen(0, 1, 2, "s")
+        warm_pe(0, 1)
+        warm_pe(1, 1)
+        load_x(xb1, 1, 1)
+        warm_pe(2, 1)
+        load_words("u", 0, E)
+        nc.vector.memset(s_raw["u"][:].bitcast(I32), 0)
+        load_scales("u")
+        nc.vector.memset(vec_rows["u"][:], 0.0)
+        load_vec("u", 0, bu, nc.sync)
+        widen(0, 0, 0, "v")
+        load_words("g", 0, E)
+        widen(0, 0, 1, "v")
+        widen(0, 0, 2, "v")
+        widen(1, 0, 2, "v")
+        load_x(xb23, 2, 2)
+        widen(0, 0, 3, "v")
+        load_y()
+        nc.vector.memset(s_raw["g"][:].bitcast(I32), 0)
+        widen(0, 1, 0, "s")
+        widen(0, 1, 1, "s")
+        load_scales("g")
+        widen(0, 1, 3, "v")
+        warm_pe(3, 1)
+        widen(1, 0, 1, "v")
+        widen(1, 1, 0, "s")
+        perm_words("u", 1, nc.vector)
+        widen(1, 1, 2, "s")
+        widen(1, 0, 3, "v")
+        turn(0, 4)
+        turn_out(0)
+        warm_pe(5, 1)
+        make_sign()
+        vec_mm("u", 6)
+        vec_out("u")
+        warm_pe(7, 1)
+        perm_scales("u", nc.vector)
+        perm_words("u", 0, nc.vector)
+        widen(1, 1, 3, "s")
+        widen(1, 1, 1, "s")
+        x_quant(0)
+        u_mm(0, 1, 0, 0)
+        widen(1, 0, 0, "v")
+        perm_words("g", 0, nc.vector)
+        u_mm(0, 0, 0, 1)
+        u_out(0, 1, 0)
+        u_out(0, 0, 0)
+        turn(1, 2)
+        u_mm(0, 0, 1, 3)
+        widen(2, 0, 2, "s")
+        turn(4, 4)
+        widen(2, 0, 0, "s")
+        turn_out(1)
+        widen(2, 0, 3, "s")
+        perm_words("g", 1, nc.vector)
+        load_vec("g", 1, gain, nc.sync)
+        turn_out(4)
+        perm_scales("g", nc.vector)
+        u_mm(0, 1, 1, 5)
+        load_vec("g", 0, bg, nc.sync)
+        x_quant(1)
+        widen(2, 1, 1, "s")
+        widen(2, 1, 0, "s")
+        widen(3, 0, 3, "s")
+        u_out(0, 0, 1)
+        u_mm(1, 0, 1, 6)
+        widen(3, 0, 1, "s")
+        u_mm(1, 0, 0, 7)
+        x_quant(4)
+        widen(2, 1, 3, "s")
+        u_mm(1, 1, 1, 0)
+        widen(2, 0, 1, "s")
+        vec_mm("g", 1)
+        vec_out("g")
+        widen(3, 0, 2, "s")
+        u_quant(0, 0)
+        u_out(1, 0, 1)
+        u_out(0, 1, 1)
+        g_mm(0, 0, 2)
+        widen(2, 1, 2, "s")
+        g_mm(0, 1, 4)
+        turn(2, 3)
+        widen(3, 1, 2, "s")
+        widen(3, 0, 0, "s")
+        u_out(1, 0, 0)
+        gelu(0, 1)
+        turn_out(2)
+        u_mm(1, 1, 0, 1)
+        gelu(0, 0)
+        u_out(1, 1, 1)
+        widen(3, 1, 0, "s")
+        g_mm(1, 1, 6)
+        u_out(1, 1, 0)
+        g_mm(1, 0, 5)
+        gelu(1, 0)
+        x_quant(2)
+        g_gain(0, nc.vector)
+        gelu(1, 1)
+        u_quant(1, 1)
+        widen(3, 1, 3, "s")
+        u_mm(2, 1, 0, 7)
+        widen(3, 1, 1, "s")
+        g_quant(0)
+        g_gain(1, nc.vector)
+        u_quant(0, 1)
+        u_mm(2, 0, 0, 4)
+        g_quant(1)
+        turn(3, 3)
+        u_mm(2, 1, 1, 2)
+        warm_pe(0, 1)
+        u_quant(1, 0)
+        s_mm(0, 1, 0, 256)
+        u_out(2, 0, 0)
+        turn_out(3)
+        x_quant(3)
+        u_mm(2, 0, 1, 5)
+        u_out(2, 1, 0)
+        u_out(2, 0, 1)
+        u_out(2, 1, 1)
+        u_quant(2, 0)
+        s_abs(0, 0, 256)
+        u_mm(3, 0, 0, 6)
+        u_quant(2, 1)
+        s_mm(1, 0, 0, 256)
+        u_out(3, 0, 0)
+        s_tanh(0, 0, 256)
+        s_abs(1, 0, 256)
+        u_mm(3, 1, 0, 4)
+        s_tanh(1, 0, 256)
+        u_mm(3, 0, 1, 3)
+        s_mm(2, 7, 0, 256)
+        s_abs(2, 0, 256)
+        u_out(3, 1, 0)
+        u_quant(3, 0, 0, 128)
+        s_tanh(2, 0, 256)
+        u_out(3, 0, 1)
+        u_mm(3, 1, 1, 5)
+        u_quant(3, 1, 0, 128)
+        u_out(3, 1, 1)
+        u_quant(3, 0, 128, 128)
+        u_quant(3, 1, 128, 128)
+        warm_pe(2, 1)
+        s_mm(3, 6, 0, 128)
+        s_mm(3, 4, 128, 128)
+        s_sign(2, 0, 256)
+        s_sign(0, 0, 256)
+        s_abs(3, 0, 128)
+        s_tanh(3, 0, 128)
+        s_sign(3, 0, 128)
+        s_sign(1, 0, 256)
+        s_abs(3, 128, 128)
+        s_sign(3, 128, 128)
+        s_tanh(3, 128, 128)
+        s_log(0, 0, 256)
+        s_finish(0, 0, 256)
+        s_log(1, 0, 256)
+        s_store(0, 0, 256)
+        s_log(2, 0, 256)
+        s_finish(1, 0, 256)
+        s_log(3, 128, 128)
+        s_finish(2, 0, 256)
+        s_finish(3, 128, 128)
+        s_store(1, 0, 256)
+        s_store(2, 0, 256)
+        s_log(3, 0, 128)
+        s_store(3, 128, 128)
+        s_finish(3, 0, 128)
+        s_store(3, 0, 128)

@@ -111,8 +111,8 @@ def tile_deepinfomaxlocalglobaljsdmap_d1p_kernel(
 
         def turn_out(h):
             nc.scalar.copy(
-                out=xt[h][:].bitcast(F32).rearrange("k (p j) -> k p j", j=4),
-                in_=held["t", h][:].rearrange("k (j p) -> k p j", j=4),
+                out=xt[h][:].bitcast(F32).rearrange("k (m i j) -> k m j i", i=2, j=4),
+                in_=held["t", h][:].rearrange("k (j m i) -> k m j i", i=2, j=4),
             )
 
         def quant(codes, scales, src):
@@ -150,9 +150,9 @@ def tile_deepinfomaxlocalglobaljsdmap_d1p_kernel(
 
         def u_out(h, g, a):
             nc.vector.tensor_tensor(
-                out=ub[h][g][:, 512 * a : 512 * (a + 1)].rearrange("p (n t) -> p n t", t=4),
-                in0=held["u", h, g, a][:].rearrange("p (t n) -> p n t", t=4),
-                in1=vec["u"][:, g, 0:4].unsqueeze(1).to_broadcast([P, 128, 4]),
+                out=ub[h][g][:, 512 * a : 512 * (a + 1)].rearrange("p (m i t) -> p m t i", i=2, t=4),
+                in0=held["u", h, g, a][:].rearrange("p (t m i) -> p m t i", i=2, t=4),
+                in1=vec["u"][:, g, 0:4].unsqueeze(1).unsqueeze(3).to_broadcast([P, 64, 4, 2]),
                 op=ALU.add,
             )
 
@@ -176,7 +176,10 @@ def tile_deepinfomaxlocalglobaljsdmap_d1p_kernel(
                 )
 
         def weave(dst, src):
-            nc.vector.tensor_copy(out=dst[:].rearrange("p (n t) -> p n t", t=4), in_=src[:].rearrange("p t n -> p n t"))
+            nc.vector.tensor_copy(
+                out=dst[:].rearrange("p (m i t) -> p m t i", i=4, t=4),
+                in_=src[:].rearrange("p t (m i) -> p m t i", i=4),
+            )
 
         def u_weave(h, g):
             weave(ub[h][g], flat["u", h, g])
@@ -209,9 +212,9 @@ def tile_deepinfomaxlocalglobaljsdmap_d1p_kernel(
 
         def g_gain(g, eng):
             eng.tensor_tensor(
-                out=gb[g][:].rearrange("p (n t) -> p n t", t=4),
-                in0=gl[g][:].rearrange("p t n -> p n t"),
-                in1=vec["g"][:, g, 4:8].unsqueeze(1).to_broadcast([P, B, 4]),
+                out=gb[g][:].rearrange("p (m i t) -> p m t i", i=2, t=4),
+                in0=gl[g][:].rearrange("p t (m i) -> p m t i", i=2),
+                in1=vec["g"][:, g, 4:8].unsqueeze(1).unsqueeze(3).to_broadcast([P, B // 2, 4, 2]),
                 op=ALU.mult,
             )
 
@@ -304,178 +307,186 @@ def tile_deepinfomaxlocalglobaljsdmap_d1p_kernel(
         def load_y():
             nc.sync.dma_start(out=yb[:].rearrange("p c k -> p (c k)"), in_=y.rearrange("(p c) k -> p (c k)", c=2))
 
+        load_x(xb0, 0, 1)
+        nc.vector.memset(s_raw["u"][:].bitcast(I32), 0)
+        nc.sync.dma_start(out=xs[:], in_=xs_rows)
+        load_x(xb1, 1, 1)
+        nc.vector.memset(half[:], 0.5)
+        load_x(xb23, 2, 2)
+        nc.vector.memset(vec_rows["u"][:], 0.0)
         nc.vector.memset(vec_rows["g"][:], 0.0)
         make_identity(nc, ident[:])
-        nc.vector.tensor_copy(out=ident_bf[:], in_=ident[:, 0:8])
-        nc.vector.memset(half[:], 0.5)
-        nc.sync.dma_start(out=xs[:], in_=xs_rows)
-        load_x(xb0, 0, 1)
+        warm_pe(0, 1)
         nc.scalar.activation(out=warm[:], in_=half[:], func=ACT.Gelu)
-        widen(0, 1, 2, "s")
-        warm_pe(0, 1)
-        warm_pe(1, 1)
-        load_x(xb1, 1, 1)
-        warm_pe(2, 1)
-        load_words("u", 0, E)
-        nc.vector.memset(s_raw["u"][:].bitcast(I32), 0)
-        load_scales("u")
-        nc.vector.memset(vec_rows["u"][:], 0.0)
-        load_vec("u", 0, bu, nc.sync)
-        widen(0, 0, 0, "v")
-        load_words("g", 0, E)
-        widen(0, 0, 1, "v")
-        widen(0, 0, 2, "v")
-        widen(1, 0, 2, "v")
-        load_x(xb23, 2, 2)
-        widen(0, 0, 3, "v")
+        load_words("u", 512, 512)
         load_y()
+        nc.vector.tensor_copy(out=ident_bf[:], in_=ident[:, 0:8])
         nc.vector.memset(s_raw["g"][:].bitcast(I32), 0)
+        widen(0, 0, 1, "v")
+        widen(0, 1, 3, "s")
+        widen(0, 0, 0, "v")
+        widen(0, 0, 3, "s")
+        widen(0, 1, 2, "s")
+        load_scales("u")
+        warm_pe(1, 1)
         widen(0, 1, 0, "s")
-        widen(0, 1, 1, "s")
-        load_scales("g")
-        widen(0, 1, 3, "v")
-        warm_pe(3, 1)
+        widen(0, 1, 1, "v")
+        widen(0, 0, 2, "v")
         widen(1, 0, 1, "v")
-        widen(1, 1, 0, "s")
-        perm_words("u", 1, nc.vector)
-        widen(1, 1, 2, "s")
-        widen(1, 0, 3, "v")
-        turn(0, 4)
-        turn_out(0)
-        warm_pe(5, 1)
-        make_sign()
-        vec_mm("u", 6)
-        vec_out("u")
-        warm_pe(7, 1)
-        perm_scales("u", nc.vector)
-        perm_words("u", 0, nc.vector)
-        widen(1, 1, 3, "s")
-        widen(1, 1, 1, "s")
-        x_quant(0)
-        u_mm(0, 1, 0, 0)
+        widen(1, 0, 2, "s")
+        widen(1, 1, 2, "v")
         widen(1, 0, 0, "v")
-        perm_words("g", 0, nc.vector)
-        u_mm(0, 0, 0, 1)
-        u_out(0, 1, 0)
-        u_out(0, 0, 0)
-        turn(1, 2)
-        u_mm(0, 0, 1, 3)
-        widen(2, 0, 2, "s")
-        turn(4, 4)
-        widen(2, 0, 0, "s")
-        turn_out(1)
-        widen(2, 0, 3, "s")
-        perm_words("g", 1, nc.vector)
-        load_vec("g", 1, gain, nc.sync)
-        turn_out(4)
-        perm_scales("g", nc.vector)
-        u_mm(0, 1, 1, 5)
-        load_vec("g", 0, bg, nc.sync)
-        x_quant(1)
-        widen(2, 1, 1, "s")
+        widen(1, 0, 3, "v")
+        widen(1, 1, 3, "v")
+        widen(3, 0, 2, "v")
+        warm_pe(2, 1)
+        widen(1, 1, 1, "s")
+        load_vec("u", 0, bu, nc.sync)
+        warm_pe(3, 1)
+        widen(3, 0, 3, "v")
+        widen(3, 1, 3, "v")
+        widen(1, 1, 0, "s")
+        load_words("u", 0, 512)
+        turn(0, 4)
         widen(2, 1, 0, "s")
-        widen(3, 0, 3, "s")
-        u_out(0, 0, 1)
-        u_mm(1, 0, 1, 6)
-        widen(3, 0, 1, "s")
-        u_mm(1, 0, 0, 7)
-        x_quant(4)
-        widen(2, 1, 3, "s")
-        u_mm(1, 1, 1, 0)
-        widen(2, 0, 1, "s")
-        vec_mm("g", 1)
-        vec_out("g")
-        widen(3, 0, 2, "s")
-        u_quant(0, 0)
-        u_out(1, 0, 1)
-        u_out(0, 1, 1)
-        g_mm(0, 0, 2)
-        widen(2, 1, 2, "s")
-        g_mm(0, 1, 4)
-        turn(2, 3)
+        widen(2, 0, 3, "s")
+        turn_out(0)
+        turn(1, 5)
+        widen(3, 1, 0, "v")
+        widen(2, 0, 2, "v")
+        turn_out(1)
+        widen(2, 0, 0, "v")
+        warm_pe(6, 1)
+        perm_words("u", 1, nc.vector)
+        warm_pe(7, 1)
         widen(3, 1, 2, "s")
-        widen(3, 0, 0, "s")
+        widen(3, 0, 0, "v")
+        turn(4, 0)
+        widen(2, 1, 2, "s")
+        widen(3, 1, 1, "v")
+        widen(2, 1, 1, "v")
+        widen(2, 1, 3, "v")
+        vec_mm("u", 1)
+        x_quant(0)
+        perm_scales("u", nc.vector)
+        widen(2, 0, 1, "s")
+        load_words("g", 0, E)
+        load_scales("g")
+        load_vec("g", 1, gain, nc.sync)
+        u_mm(0, 1, 1, 2)
+        x_quant(1)
+        vec_out("u")
+        u_mm_wide(1, 1, 0, 3)
+        widen(3, 0, 1, "v")
+        u_mm_wide(1, 1, 1, 4)
+        turn_out(4)
+        perm_words("u", 0, nc.vector)
+        u_out(0, 1, 1)
+        u_bias(1, 1, 0)
+        make_sign()
+        u_mm(1, 0, 0, 5)
+        x_quant(4)
+        load_vec("g", 0, bg, nc.sync)
+        perm_words("g", 0, nc.vector)
+        turn(3, 6)
         u_out(1, 0, 0)
-        gelu(0, 1)
-        turn_out(2)
-        u_mm(1, 1, 0, 1)
-        gelu(0, 0)
-        u_out(1, 1, 1)
-        widen(3, 1, 0, "s")
-        g_mm(1, 1, 6)
-        u_out(1, 1, 0)
-        g_mm(1, 0, 5)
-        gelu(1, 0)
-        x_quant(2)
-        g_gain(0, nc.vector)
-        gelu(1, 1)
-        u_quant(1, 1)
-        widen(3, 1, 3, "s")
-        u_mm(2, 1, 0, 7)
-        widen(3, 1, 1, "s")
-        g_quant(0)
-        g_gain(1, nc.vector)
-        u_quant(0, 1)
-        u_mm(2, 0, 0, 4)
-        g_quant(1)
-        turn(3, 3)
-        u_mm(2, 1, 1, 2)
-        warm_pe(0, 1)
-        u_quant(1, 0)
-        s_mm(0, 1, 0, 256)
-        u_out(2, 0, 0)
+        turn(2, 7)
+        u_mm(1, 0, 1, 1)
+        u_bias(1, 1, 1)
+        perm_scales("g", nc.vector)
+        vec_mm("g", 0)
+        g_mm(0, 0, 2)
         turn_out(3)
+        u_mm(0, 0, 0, 3)
+        g_mm(0, 1, 5)
+        u_weave(1, 1)
+        turn_out(2)
+        vec_out("g")
+        u_mm(0, 0, 1, 4)
+        gelu(0, 0)
         x_quant(3)
-        u_mm(2, 0, 1, 5)
-        u_out(2, 1, 0)
-        u_out(2, 0, 1)
-        u_out(2, 1, 1)
-        u_quant(2, 0)
-        s_abs(0, 0, 256)
-        u_mm(3, 0, 0, 6)
-        u_quant(2, 1)
-        s_mm(1, 0, 0, 256)
-        u_out(3, 0, 0)
-        s_tanh(0, 0, 256)
-        s_abs(1, 0, 256)
-        u_mm(3, 1, 0, 4)
-        s_tanh(1, 0, 256)
-        u_mm(3, 0, 1, 3)
-        s_mm(2, 7, 0, 256)
-        s_abs(2, 0, 256)
+        u_mm(3, 1, 0, 6)
+        perm_words("g", 1, nc.vector)
+        gelu(0, 1)
+        x_quant(2)
+        g_scale(0, 0)
+        u_mm(3, 1, 1, 7)
+        g_mm(1, 1, 0)
+        u_out(1, 0, 1)
+        g_mm(1, 0, 2)
+        u_out(0, 0, 0)
+        u_mm(3, 0, 1, 5)
+        u_out(0, 0, 1)
+        u_mm(0, 1, 0, 1)
+        gelu(1, 1)
+        u_mm(3, 0, 0, 3)
+        u_mm_wide(2, 1, 1, 4)
         u_out(3, 1, 0)
-        u_quant(3, 0, 0, 128)
-        s_tanh(2, 0, 256)
-        u_out(3, 0, 1)
-        u_mm(3, 1, 1, 5)
+        u_mm_wide(2, 1, 0, 0)
+        u_mm_wide(2, 0, 1, 6)
+        g_scale(0, 1)
+        u_quant(1, 1)
+        u_quant(0, 0)
+        u_quant(1, 0)
+        gelu(1, 0)
         u_quant(3, 1, 0, 128)
+        u_mm_wide(2, 0, 0, 2)
+        u_out(0, 1, 0)
+        g_scale(1, 1)
+        g_scale(1, 0)
+        u_bias(2, 0, 0)
+        g_weave(0)
+        g_weave(1)
+        g_quant(0)
+        u_bias(2, 1, 0)
+        warm_pe(1, 1)
+        g_quant(1)
+        warm_pe(2, 1)
+        u_quant(0, 1)
+        u_bias(2, 0, 1)
+        u_out(3, 0, 0)
+        s_mm(1, 0, 0, 256)
+        s_mm(0, 1, 0, 256)
+        u_bias(2, 1, 1)
+        s_abs(1, 0, 256)
+        s_abs(0, 0, 256)
+        u_weave(2, 0)
+        s_tanh(1, 0, 256)
+        u_quant(3, 0, 0, 128)
+        u_weave(2, 1)
+        s_mm(3, 2, 0, 128)
+        s_abs(3, 0, 128)
+        u_quant(2, 0)
+        s_tanh(0, 0, 256)
+        u_quant(2, 1)
+        s_tanh(3, 0, 128)
+        u_out(3, 0, 1)
+        s_mm(2, 6, 0, 256)
         u_out(3, 1, 1)
         u_quant(3, 0, 128, 128)
+        s_abs(2, 0, 256)
         u_quant(3, 1, 128, 128)
-        warm_pe(2, 1)
-        s_mm(3, 6, 0, 128)
-        s_mm(3, 4, 128, 128)
-        s_sign(2, 0, 256)
-        s_sign(0, 0, 256)
-        s_abs(3, 0, 128)
-        s_tanh(3, 0, 128)
+        s_tanh(2, 0, 256)
+        s_mm(3, 3, 128, 128)
         s_sign(3, 0, 128)
-        s_sign(1, 0, 256)
+        s_sign(2, 0, 256)
         s_abs(3, 128, 128)
-        s_sign(3, 128, 128)
         s_tanh(3, 128, 128)
+        s_sign(1, 0, 256)
+        s_sign(3, 128, 128)
+        s_sign(0, 0, 256)
         s_log(0, 0, 256)
         s_finish(0, 0, 256)
         s_log(1, 0, 256)
         s_store(0, 0, 256)
         s_log(2, 0, 256)
         s_finish(1, 0, 256)
-        s_log(3, 128, 128)
         s_finish(2, 0, 256)
-        s_finish(3, 128, 128)
         s_store(1, 0, 256)
-        s_store(2, 0, 256)
         s_log(3, 0, 128)
-        s_store(3, 128, 128)
+        s_log(3, 128, 128)
+        s_finish(3, 128, 128)
+        s_store(2, 0, 256)
         s_finish(3, 0, 128)
+        s_store(3, 128, 128)
         s_store(3, 0, 128)

@@ -47,19 +47,22 @@ def tile_deepinfomaxlocalglobaljsdmap_d1p_kernel(
         xw = [[keep("xw%d_%d" % (h, c), [P, D], BF16) for c in range(2)] for h in range(GROUPS)]
         yb = keep("yb", [P, 2, D], BF16)
         xt = [keep("xt%d" % h, [P, 4 * TOK], BF16) for h in range(GROUPS + 1)]
-        xq = [keep("xq%d" % h, [P, TOK], U32) for h in range(GROUPS + 1)]
-        xqs = [keep("xqs%d" % h, [P, TOK], U8) for h in range(GROUPS + 1)]
+        xq_all = keep("xq_all", [P, (GROUPS + 1) * TOK], U32)
+        xqs_all = keep("xqs_all", [P, (GROUPS + 1) * TOK], U8)
+        xq = [xq_all[:, TOK * h : TOK * (h + 1)] for h in range(GROUPS + 1)]
+        xqs = [xqs_all[:, TOK * h : TOK * (h + 1)] for h in range(GROUPS + 1)]
         w_raw = {w: keep("wraw_%s" % w, [P, E], U32) for w in "ug"}
         w_perm = {(w, g): keep("wperm_%s%d" % (w, g), [P, 512], U32) for w in "ug" for g in range(2)}
         s_raw = {w: keep("sraw_%s" % w, [P, E], U8) for w in "ug"}
         s_perm = {w: keep("sperm_%s" % w, [P, E], U8) for w in "ug"}
-        vec_rows = {w: keep("vec_rows_%s" % w, [P, 256], BF16) for w in "ug"}
-        vec = {w: keep("vec_%s" % w, [P, 2, 8], F32) for w in "ug"}
+        vec_rows = keep("vec_rows", [4, E], BF16)
+        vec_perm = keep("vec_perm", [P, E], BF16)
+        vec = keep("vec", [P, 3, 2, 4], F32)
         ident = keep("ident", [P, P], F32)
         ident_bf = keep("ident_bf", [P, 8], BF16)
         half = keep("half", [P, 1], F32)
         warm = keep("warm", [P, 1], F32)
-        sign = keep("sign", [P, 4, 64], F32)
+        sign = keep("sign", [P, P], F32)
         ub = [[keep("ub%d_%d" % (h, g), [P, 4 * TOK], BF16) for g in range(2)] for h in range(GROUPS)]
         uq = [[keep("uq%d_%d" % (h, g), [P, TOK], U32) for g in range(2)] for h in range(GROUPS)]
         uqs = [[keep("uqs%d_%d" % (h, g), [P, TOK], U8) for g in range(2)] for h in range(GROUPS)]
@@ -69,13 +72,17 @@ def tile_deepinfomaxlocalglobaljsdmap_d1p_kernel(
         gqs = [keep("gqs%d" % g, [P, B], U8) for g in range(2)]
         PIECES = ((0, 0, 256), (1, 0, 256), (2, 0, 256), (3, 0, 128), (3, 128, 128))
         th = {(h, lo): keep("th%d_%d" % (h, lo), [P, 2, n], F32) for h, lo, n in PIECES}
+        sg = {(h, lo): keep("sg%d_%d" % (h, lo), [P, 2, n], F32) for h, lo, n in PIECES}
         lg = {(h, lo): keep("lg%d_%d" % (h, lo), [P, 2, n], F32) for h, lo, n in PIECES}
-        r = {(h, lo): keep("r%d_%d" % (h, lo), [P, 2, n], F32) for h, lo, n in PIECES}
+        r = {(h, lo): keep("r%d_%d" % (h, lo), [P, n], F32) for h, lo, n in PIECES}
         res = {(h, lo): keep("res%d_%d" % (h, lo), [P, 2, n], F32) for h, lo, n in PIECES}
 
         flat = {("u", h, g): keep("flat_u%d_%d" % (h, g), [P, 4, TOK], BF16) for h in range(GROUPS) for g in range(2)}
         flat.update({("g", g): keep("flat_g%d" % g, [P, 4, B], BF16) for g in range(2)})
 
+        wide = [keep("wide%d" % g, [P, 4, 2 * TOK], BF16) for g in range(2)]
+
+        gain_col = [keep("gain_col%d" % g, [P, 4], F32) for g in range(2)]
         words_in = {"u": wu_words, "g": wg_words}
         scales_in = {"u": wu_scales, "g": wg_scales}
         held = {}
@@ -136,8 +143,8 @@ def tile_deepinfomaxlocalglobaljsdmap_d1p_kernel(
                 out=dst,
                 lhsT=w_perm[w, g][:, 128 * t : 128 * (t + 1)].bitcast(FP8X4),
                 lhsT_scale=s_perm[w][:, 256 * t + 128 * g : 256 * t + 128 * (g + 1)],
-                rhs=xq[h][:, cols].bitcast(FP8X4),
-                rhs_scale=xqs[h][:, cols],
+                rhs=xq_all[:, TOK * h + cols.start : TOK * h + cols.stop].bitcast(FP8X4),
+                rhs_scale=xqs_all[:, TOK * h + cols.start : TOK * h + cols.stop],
                 start=True,
                 stop=True,
             )
@@ -152,14 +159,14 @@ def tile_deepinfomaxlocalglobaljsdmap_d1p_kernel(
             nc.vector.tensor_tensor(
                 out=ub[h][g][:, 512 * a : 512 * (a + 1)].rearrange("p (m i t) -> p m t i", i=2, t=4),
                 in0=held["u", h, g, a][:].rearrange("p (t m i) -> p m t i", i=2, t=4),
-                in1=vec["u"][:, g, 0:4].unsqueeze(1).unsqueeze(3).to_broadcast([P, 64, 4, 2]),
+                in1=vec[:, 0, g, :].unsqueeze(1).unsqueeze(3).to_broadcast([P, 64, 4, 2]),
                 op=ALU.add,
             )
 
         def u_quant(h, g, lo=0, n=TOK):
             quant(uq[h][g][:, lo : lo + n], uqs[h][g][:, lo : lo + n], ub[h][g][:, 4 * lo : 4 * (lo + n)])
 
-        def u_mm_wide(h, g, a, k):
+        def u_mm_pair(h, g, a, k):
             t = bank(k)
             held["u", h, g, a] = t
             for j in range(2):
@@ -172,11 +179,24 @@ def tile_deepinfomaxlocalglobaljsdmap_d1p_kernel(
                     out=flat["u", h, g][:, t, :],
                     in_=held["u", h, g, a][:, 256 * j : 256 * (j + 1)],
                     func=ACT.Identity,
-                    bias=vec["u"][:, g, t : t + 1],
+                    bias=vec[:, 0, g, t : t + 1],
                 )
 
-        def weave(dst, src):
-            nc.vector.tensor_copy(
+        def u_mm_wide(g, t, k):
+            b = bank(k)
+            held["w", g, t] = b
+            first_mm(b[:], "u", g, t, 1, slice(0, 2 * TOK))
+
+        def u_bias_wide(g, t):
+            nc.scalar.activation(
+                out=wide[g][:, t, :], in_=held["w", g, t][:], func=ACT.Identity, bias=vec[:, 0, g, t : t + 1]
+            )
+
+        def u_weave_wide(h, g, eng):
+            weave(ub[h][g], wide[g][:, :, TOK * (h - 1) : TOK * h], eng)
+
+        def weave(dst, src, eng=nc.vector):
+            eng.tensor_copy(
                 out=dst[:].rearrange("p (m i t) -> p m t i", i=4, t=4),
                 in_=src[:].rearrange("p t (m i) -> p m t i", i=4),
             )
@@ -188,7 +208,7 @@ def tile_deepinfomaxlocalglobaljsdmap_d1p_kernel(
             for j in range(2):
                 t = 2 * a + j
                 nc.scalar.activation(
-                    out=flat["g", g][:, t, :], in_=gl[g][:, t, :], func=ACT.Copy, scale=vec["g"][:, g, 4 + t : 5 + t]
+                    out=flat["g", g][:, t, :], in_=gl[g][:, t, :], func=ACT.Copy, scale=vec[:, 2, g, t : t + 1]
                 )
 
         def g_weave(g):
@@ -207,37 +227,52 @@ def tile_deepinfomaxlocalglobaljsdmap_d1p_kernel(
                     out=gl[g][:, t, :],
                     in_=held["g", g, a][:, 256 * j : 256 * (j + 1)],
                     func=ACT.Gelu,
-                    bias=vec["g"][:, g, t : t + 1],
+                    bias=vec[:, 1, g, t : t + 1],
                 )
+
+        def gate(g):
+            nc.vector.tensor_copy(out=gain_col[g][:], in_=vec[:, 2, g, :])
+
+        def g_gain_pool(g):
+            nc.gpsimd.tensor_tensor(
+                out=gb[g][:].rearrange("p (n t) -> p n t", t=4),
+                in0=gl[g][:].rearrange("p t n -> p n t"),
+                in1=gain_col[g][:].unsqueeze(1).to_broadcast([P, B, 4]),
+                op=ALU.mult,
+            )
 
         def g_gain(g, eng):
             eng.tensor_tensor(
                 out=gb[g][:].rearrange("p (m i t) -> p m t i", i=2, t=4),
                 in0=gl[g][:].rearrange("p t (m i) -> p m t i", i=2),
-                in1=vec["g"][:, g, 4:8].unsqueeze(1).unsqueeze(3).to_broadcast([P, B // 2, 4, 2]),
+                in1=vec[:, 2, g, :].unsqueeze(1).unsqueeze(3).to_broadcast([P, B // 2, 4, 2]),
                 op=ALU.mult,
             )
 
         def load_words(w, lo, n):
             nc.sync.dma_start(out=w_raw[w][:, lo : lo + n].bitcast(I32), in_=words(w)[:, lo : lo + n])
 
-        def load_vec(w, v, src, eng):
-            eng.dma_start(
-                out=vec_rows[w][4 * v : 4 * v + 4, :].rearrange("t (m r) -> t m r", r=8),
-                in_=src.rearrange("(m t r) -> t m r", t=4, r=8),
+        def load_vec(v, src):
+            nc.sync.dma_start(out=vec_rows[v : v + 1, :], in_=src.unsqueeze(0))
+
+        def perm_vec():
+            nc.vector.tensor_copy(
+                out=vec_perm[0:3, :].rearrange("p (t m r) -> p t m r", t=4, r=8),
+                in_=vec_rows[0:3, :].rearrange("p (m t r) -> p t m r", t=4, r=8),
             )
 
-        def vec_mm(w, k):
+        def vec_mm(k):
             t = bank(k)
-            held["v", w] = t
-            for g in range(2):
+            held["v"] = t
+            for j in range(8):
                 nc.tensor.matmul(
-                    t[:, 8 * g : 8 * (g + 1)], lhsT=vec_rows[w][:, 128 * g : 128 * (g + 1)], rhs=ident_bf[:],
+                    t[:, 4 * j : 4 * (j + 1)], lhsT=vec_perm[:, 128 * j : 128 * (j + 1)], rhs=ident_bf[:, 0:4],
                     start=True, stop=True,
                 )
 
-        def vec_out(w):
-            nc.scalar.copy(out=vec[w][:].rearrange("p g v -> p (g v)"), in_=held["v", w][:, 0:16])
+        def vec_out():
+            for g in range(1):
+                nc.scalar.copy(out=vec[:], in_=held["v"][:, 0:32].rearrange("p (t g v) -> p v g t", t=4, g=2)[:, 0:3])
 
         def warm_pe(k, n):
             t = bank(k)
@@ -261,28 +296,50 @@ def tile_deepinfomaxlocalglobaljsdmap_d1p_kernel(
 
         def s_abs(h, lo=0, n=TOK):
             src = held["s", h, lo][:, 0 : 2 * n].rearrange("p (a n) -> p a n", a=2)
-            nc.scalar.activation(out=th[h, lo][:], in_=src, func=ACT.Abs, scale=1.0 / 32.0)
+            nc.scalar.activation(out=th[h, lo][:], in_=src, func=ACT.Abs, scale=0.5)
 
         def s_tanh(h, lo=0, n=TOK):
             nc.scalar.activation(out=th[h, lo][:], in_=th[h, lo][:], func=ACT.Tanh)
 
-        def s_sign(h, lo=0, n=TOK):
-            pick = [sign[:, 1:4:2, :], sign[:, 2:4, :], sign[:, 0:2, :], sign[:, 0:3:2, :]][h]
+        def s_tanh_first(h, lo, n):
+            src = held["s", h, lo][:, 0 : 2 * n].rearrange("p (a n) -> p a n", a=2)
+            nc.scalar.activation(out=sg[h, lo][:], in_=src, func=ACT.Tanh, scale=0.5)
+
+        def s_abs_after(h, lo, n):
+            nc.vector.scalar_tensor_tensor(
+                out=th[h, lo][:], in0=sg[h, lo][:], scalar=-1.0, in1=sg[h, lo][:], op0=ALU.mult, op1=ALU.max
+            )
+
+        def s_sign(h, lo, n):
+            a = h // 2
+            j0 = 64 * (h % 2) + lo // L
             nc.vector.tensor_tensor(
-                out=r[h, lo][:].rearrange("p a (j l) -> p a j l", l=L),
-                in0=held["s", h, lo][:, 0 : 2 * n].rearrange("p (a j l) -> p a j l", a=2, l=L),
-                in1=pick[:, :, lo // L : (lo + n) // L].unsqueeze(3).to_broadcast([P, 2, n // L, L]),
+                out=r[h, lo][:].rearrange("p (j l) -> p j l", l=L),
+                in0=held["s", h, lo][:, n * a : n * (a + 1)].rearrange("p (j l) -> p j l", l=L),
+                in1=sign[:, j0 : j0 + n // L].unsqueeze(2).to_broadcast([P, n // L, L]),
                 op=ALU.mult,
+            )
+
+        def finish(h, lo, a, src):
+            nc.vector.scalar_tensor_tensor(
+                out=res[h, lo][:, a, :], in0=src, scalar=0.0, in1=lg[h, lo][:, a, :], op0=ALU.max, op1=ALU.subtract
+            )
+
+        def finish_plain(h, lo, n):
+            a = 1 - h // 2
+            finish(h, lo, a, held["s", h, lo][:, n * a : n * (a + 1)])
+
+        def finish_diag(h, lo, n):
+            finish(h, lo, h // 2, r[h, lo][:])
+
+        def make_pick():
+            nc.vector.tensor_copy(out=ident_bf[:], in_=ident[:, 0:8])
+            nc.vector.tensor_scalar(
+                out=ident_bf[:, 2:4], in0=ident[:, 2:4], scalar1=1.0 / 16.0, scalar2=None, op0=ALU.mult
             )
 
         def s_log(h, lo=0, n=TOK):
             nc.scalar.activation(out=lg[h, lo][:], in_=th[h, lo][:], func=ACT.Ln, scale=0.5, bias=half[:])
-
-        def s_finish(h, lo=0, n=TOK):
-            nc.vector.scalar_tensor_tensor(
-                out=res[h, lo][:], in0=r[h, lo][:], scalar=0.0, in1=lg[h, lo][:],
-                op0=ALU.max, op1=ALU.subtract,
-            )
 
         def s_store(h, lo, n):
             nc.sync.dma_start(out=out_rows[:, :, TOK * h + lo : TOK * h + lo + n], in_=res[h, lo][:])
@@ -294,10 +351,9 @@ def tile_deepinfomaxlocalglobaljsdmap_d1p_kernel(
             quant(gq[g], gqs[g], gb[g])
 
         def make_sign():
-            nc.gpsimd.memset(sign[:], 1.0 / 16.0)
-            diag = sign[:].rearrange("p a j -> p (a j)")[:, 64:192]
+            nc.gpsimd.memset(sign[:], 1.0)
             nc.gpsimd.affine_select(
-                out=diag, in_=diag, pattern=[[-1, P]], compare_op=ALU.not_equal, fill=-1.0 / 16.0, base=0,
+                out=sign[:], in_=sign[:], pattern=[[-1, P]], compare_op=ALU.not_equal, fill=-1.0, base=0,
                 channel_multiplier=1,
             )
 
@@ -307,186 +363,189 @@ def tile_deepinfomaxlocalglobaljsdmap_d1p_kernel(
         def load_y():
             nc.sync.dma_start(out=yb[:].rearrange("p c k -> p (c k)"), in_=y.rearrange("(p c) k -> p (c k)", c=2))
 
-        load_x(xb0, 0, 1)
-        nc.vector.memset(s_raw["u"][:].bitcast(I32), 0)
+        make_identity(nc, ident[:])
+        make_sign()
         nc.sync.dma_start(out=xs[:], in_=xs_rows)
         load_x(xb1, 1, 1)
-        nc.vector.memset(half[:], 0.5)
+        load_x(xb0, 0, 1)
+        load_vec(2, gain)
         load_x(xb23, 2, 2)
-        nc.vector.memset(vec_rows["u"][:], 0.0)
-        nc.vector.memset(vec_rows["g"][:], 0.0)
-        make_identity(nc, ident[:])
-        warm_pe(0, 1)
-        nc.scalar.activation(out=warm[:], in_=half[:], func=ACT.Gelu)
-        load_words("u", 512, 512)
+        load_vec(1, bg)
         load_y()
-        nc.vector.tensor_copy(out=ident_bf[:], in_=ident[:, 0:8])
-        nc.vector.memset(s_raw["g"][:].bitcast(I32), 0)
-        widen(0, 0, 1, "v")
-        widen(0, 1, 3, "s")
-        widen(0, 0, 0, "v")
-        widen(0, 0, 3, "s")
-        widen(0, 1, 2, "s")
-        load_scales("u")
-        warm_pe(1, 1)
-        widen(0, 1, 0, "s")
-        widen(0, 1, 1, "v")
-        widen(0, 0, 2, "v")
-        widen(1, 0, 1, "v")
-        widen(1, 0, 2, "s")
-        widen(1, 1, 2, "v")
-        widen(1, 0, 0, "v")
-        widen(1, 0, 3, "v")
-        widen(1, 1, 3, "v")
-        widen(3, 0, 2, "v")
-        warm_pe(2, 1)
-        widen(1, 1, 1, "s")
-        load_vec("u", 0, bu, nc.sync)
-        warm_pe(3, 1)
-        widen(3, 0, 3, "v")
-        widen(3, 1, 3, "v")
-        widen(1, 1, 0, "s")
+        load_vec(0, bu)
         load_words("u", 0, 512)
-        turn(0, 4)
-        widen(2, 1, 0, "s")
-        widen(2, 0, 3, "s")
-        turn_out(0)
-        turn(1, 5)
-        widen(3, 1, 0, "v")
-        widen(2, 0, 2, "v")
-        turn_out(1)
-        widen(2, 0, 0, "v")
-        warm_pe(6, 1)
-        perm_words("u", 1, nc.vector)
-        warm_pe(7, 1)
-        widen(3, 1, 2, "s")
-        widen(3, 0, 0, "v")
-        turn(4, 0)
-        widen(2, 1, 2, "s")
-        widen(3, 1, 1, "v")
-        widen(2, 1, 1, "v")
+        nc.vector.memset(vec_perm[:], 0.0)
+        nc.vector.memset(half[:], 0.5)
+        nc.vector.memset(s_raw["g"][:].bitcast(I32), 0)
+        nc.vector.memset(s_raw["u"][:].bitcast(I32), 0)
+        load_scales("u")
+        load_words("u", 512, 512)
+        nc.scalar.activation(out=warm[:], in_=half[:], func=ACT.Gelu)
+        widen(0, 1, 0, "v")
+        widen(0, 1, 3, "v")
+        make_pick()
+        widen(1, 1, 2, "v")
+        widen(0, 1, 2, "v")
+        widen(1, 1, 1, "v")
+        widen(0, 0, 0, "v")
+        widen(2, 0, 1, "v")
         widen(2, 1, 3, "v")
-        vec_mm("u", 1)
-        x_quant(0)
+        widen(3, 0, 0, "v")
+        widen(2, 1, 2, "v")
+        widen(3, 1, 1, "v")
+        widen(0, 1, 1, "v")
+        perm_vec()
+        widen(3, 0, 2, "v")
+        widen(2, 0, 3, "v")
+        perm_words("u", 0, nc.vector)
+        widen(1, 1, 0, "s")
+        widen(1, 0, 3, "s")
+        widen(1, 0, 0, "s")
+        widen(1, 0, 1, "s")
+        widen(1, 0, 2, "s")
+        widen(1, 1, 3, "s")
+        widen(2, 1, 0, "s")
+        widen(0, 0, 2, "s")
+        widen(0, 0, 3, "s")
+        widen(2, 0, 2, "s")
+        widen(0, 0, 1, "s")
+        warm_pe(0, 1)
+        warm_pe(1, 1)
+        warm_pe(2, 1)
+        warm_pe(3, 1)
+        warm_pe(4, 1)
+        warm_pe(5, 1)
+        turn(1, 6)
+        turn(4, 7)
+        turn_out(1)
+        turn(0, 0)
+        turn_out(4)
+        x_quant(1)
         perm_scales("u", nc.vector)
-        widen(2, 0, 1, "s")
+        turn_out(0)
+        vec_mm(1)
+        vec_out()
+        u_mm(1, 0, 0, 2)
+        widen(2, 1, 1, "s")
+        widen(3, 1, 2, "s")
+        widen(3, 0, 3, "s")
+        u_mm(1, 0, 1, 3)
+        widen(3, 1, 3, "s")
+        widen(3, 0, 1, "s")
+        widen(3, 1, 0, "s")
+        widen(2, 0, 0, "s")
+        x_quant(4)
+        perm_words("u", 1, nc.vector)
+        x_quant(0)
         load_words("g", 0, E)
         load_scales("g")
-        load_vec("g", 1, gain, nc.sync)
-        u_mm(0, 1, 1, 2)
-        x_quant(1)
-        vec_out("u")
-        u_mm_wide(1, 1, 0, 3)
-        widen(3, 0, 1, "v")
-        u_mm_wide(1, 1, 1, 4)
-        turn_out(4)
-        perm_words("u", 0, nc.vector)
-        u_out(0, 1, 1)
-        u_bias(1, 1, 0)
-        make_sign()
-        u_mm(1, 0, 0, 5)
-        x_quant(4)
-        load_vec("g", 0, bg, nc.sync)
-        perm_words("g", 0, nc.vector)
-        turn(3, 6)
+        u_mm_pair(1, 1, 0, 4)
+        turn(3, 5)
         u_out(1, 0, 0)
-        turn(2, 7)
-        u_mm(1, 0, 1, 1)
-        u_bias(1, 1, 1)
-        perm_scales("g", nc.vector)
-        vec_mm("g", 0)
-        g_mm(0, 0, 2)
-        turn_out(3)
-        u_mm(0, 0, 0, 3)
-        g_mm(0, 1, 5)
-        u_weave(1, 1)
-        turn_out(2)
-        vec_out("g")
-        u_mm(0, 0, 1, 4)
-        gelu(0, 0)
-        x_quant(3)
-        u_mm(3, 1, 0, 6)
-        perm_words("g", 1, nc.vector)
-        gelu(0, 1)
-        x_quant(2)
-        g_scale(0, 0)
-        u_mm(3, 1, 1, 7)
-        g_mm(1, 1, 0)
+        u_bias(1, 1, 0)
         u_out(1, 0, 1)
-        g_mm(1, 0, 2)
-        u_out(0, 0, 0)
-        u_mm(3, 0, 1, 5)
-        u_out(0, 0, 1)
-        u_mm(0, 1, 0, 1)
-        gelu(1, 1)
-        u_mm(3, 0, 0, 3)
-        u_mm_wide(2, 1, 1, 4)
-        u_out(3, 1, 0)
-        u_mm_wide(2, 1, 0, 0)
-        u_mm_wide(2, 0, 1, 6)
-        g_scale(0, 1)
-        u_quant(1, 1)
-        u_quant(0, 0)
+        perm_words("g", 0, nc.vector)
+        u_mm(0, 0, 0, 6)
+        perm_scales("g", nc.vector)
+        perm_words("g", 1, nc.vector)
         u_quant(1, 0)
-        gelu(1, 0)
-        u_quant(3, 1, 0, 128)
-        u_mm_wide(2, 0, 0, 2)
+        u_mm_pair(1, 1, 1, 7)
+        g_mm(0, 0, 0)
+        turn_out(3)
+        g_mm(1, 1, 1)
+        g_mm(0, 1, 2)
+        u_out(0, 0, 0)
+        u_mm(0, 1, 1, 4)
+        x_quant(3)
+        g_mm(1, 0, 3)
+        u_bias(1, 1, 1)
+        u_weave(1, 1)
+        u_out(0, 1, 1)
+        u_mm(0, 1, 0, 5)
+        u_mm(0, 0, 1, 6)
+        turn(2, 7)
+        u_out(0, 0, 1)
+        u_mm(3, 1, 1, 4)
         u_out(0, 1, 0)
+        gelu(1, 1)
+        gelu(0, 1)
+        gelu(0, 0)
+        u_mm(3, 0, 0, 6)
+        warm_pe(5, 1)
+        u_quant(1, 1)
+        u_quant(0, 1)
+        u_out(3, 1, 1)
+        turn_out(2)
+        gelu(1, 0)
+        x_quant(2)
+        g_scale(0, 1)
+        g_scale(0, 0)
+        u_quant(3, 1, 128, 128)
+        u_quant(0, 0)
         g_scale(1, 1)
         g_scale(1, 0)
-        u_bias(2, 0, 0)
         g_weave(0)
+        u_out(3, 0, 0)
         g_weave(1)
         g_quant(0)
-        u_bias(2, 1, 0)
-        warm_pe(1, 1)
         g_quant(1)
-        warm_pe(2, 1)
-        u_quant(0, 1)
-        u_bias(2, 0, 1)
-        u_out(3, 0, 0)
-        s_mm(1, 0, 0, 256)
-        s_mm(0, 1, 0, 256)
-        u_bias(2, 1, 1)
-        s_abs(1, 0, 256)
-        s_abs(0, 0, 256)
-        u_weave(2, 0)
-        s_tanh(1, 0, 256)
-        u_quant(3, 0, 0, 128)
-        u_weave(2, 1)
-        s_mm(3, 2, 0, 128)
-        s_abs(3, 0, 128)
-        u_quant(2, 0)
-        s_tanh(0, 0, 256)
-        u_quant(2, 1)
-        s_tanh(3, 0, 128)
+        u_mm(3, 0, 1, 1)
         u_out(3, 0, 1)
-        s_mm(2, 6, 0, 256)
-        u_out(3, 1, 1)
+        u_mm_pair(2, 0, 1, 2)
+        u_mm_pair(2, 0, 0, 0)
+        u_bias(2, 0, 1)
+        u_mm_pair(2, 1, 1, 5)
+        u_bias(2, 0, 0)
+        u_mm_pair(2, 1, 0, 4)
+        warm_pe(7, 1)
+        u_weave(2, 0)
+        u_bias(2, 1, 1)
+        u_bias(2, 1, 0)
+        u_mm(3, 1, 0, 3)
+        u_weave(2, 1)
+        u_quant(2, 0)
+        u_quant(2, 1)
+        s_mm(1, 6, 0, 256)
+        s_abs(1, 0, 256)
+        s_mm(0, 1, 0, 256)
+        s_mm(2, 2, 0, 256)
+        u_out(3, 1, 0)
         u_quant(3, 0, 128, 128)
-        s_abs(2, 0, 256)
-        u_quant(3, 1, 128, 128)
-        s_tanh(2, 0, 256)
-        s_mm(3, 3, 128, 128)
+        s_mm(3, 0, 128, 128)
+        s_abs(0, 0, 256)
+        s_tanh(1, 0, 256)
+        s_tanh(0, 0, 256)
+        u_quant(3, 0, 0, 128)
+        u_quant(3, 1, 0, 128)
+        s_tanh_first(2, 0, 256)
+        s_tanh_first(3, 128, 128)
+        s_sign(1, 0, 256)
+        s_mm(3, 7, 0, 128)
+        s_sign(0, 0, 256)
+        s_tanh_first(3, 0, 128)
+        s_abs_after(2, 0, 256)
+        s_abs_after(3, 128, 128)
+        s_abs_after(3, 0, 128)
+        s_sign(3, 128, 128)
+        s_log(3, 0, 128)
         s_sign(3, 0, 128)
         s_sign(2, 0, 256)
-        s_abs(3, 128, 128)
-        s_tanh(3, 128, 128)
-        s_sign(1, 0, 256)
-        s_sign(3, 128, 128)
-        s_sign(0, 0, 256)
-        s_log(0, 0, 256)
-        s_finish(0, 0, 256)
-        s_log(1, 0, 256)
-        s_store(0, 0, 256)
-        s_log(2, 0, 256)
-        s_finish(1, 0, 256)
-        s_finish(2, 0, 256)
-        s_store(1, 0, 256)
-        s_log(3, 0, 128)
+        finish_plain(3, 0, 128)
+        finish_diag(3, 0, 128)
         s_log(3, 128, 128)
-        s_finish(3, 128, 128)
-        s_store(2, 0, 256)
-        s_finish(3, 0, 128)
-        s_store(3, 128, 128)
+        finish_diag(3, 128, 128)
+        finish_plain(3, 128, 128)
+        s_log(0, 0, 256)
+        finish_diag(0, 0, 256)
+        finish_plain(0, 0, 256)
+        s_log(1, 0, 256)
+        s_log(2, 0, 256)
+        finish_plain(1, 0, 256)
+        finish_diag(1, 0, 256)
+        finish_plain(2, 0, 256)
+        finish_diag(2, 0, 256)
         s_store(3, 0, 128)
+        s_store(3, 128, 128)
+        s_store(0, 0, 256)
+        s_store(1, 0, 256)
+        s_store(2, 0, 256)

@@ -17,6 +17,7 @@ B, L, D, E = 256, 4, 512, 1024
 P = 128
 GROUPS = 4
 TOK = 256
+HI = ((0, 256), (256, 128), (384, 128))
 FLOPS = 2 * (B * L * D * E + B * D * E + B * E * B * L)
 
 
@@ -63,26 +64,32 @@ def tile_deepinfomaxlocalglobaljsdmap_d1p_kernel(
         half = keep("half", [P, 1], F32)
         warm = keep("warm", [P, 1], F32)
         sign = keep("sign", [P, P], F32)
-        ub = [[keep("ub%d_%d" % (h, g), [P, 4 * TOK], BF16) for g in range(2)] for h in range(GROUPS)]
-        uq = [[keep("uq%d_%d" % (h, g), [P, TOK], U32) for g in range(2)] for h in range(GROUPS)]
-        uqs = [[keep("uqs%d_%d" % (h, g), [P, TOK], U8) for g in range(2)] for h in range(GROUPS)]
+        ub_all = [keep("ub%d" % h, [P, 2 * 4 * TOK], BF16) for h in range(GROUPS)]
+        uq_all = [keep("uq%d" % h, [P, 2 * TOK], U32) for h in range(GROUPS)]
+        uqs_all = [keep("uqs%d" % h, [P, 2 * TOK], U8) for h in range(GROUPS)]
+        ub = [[t[:, 4 * TOK * g : 4 * TOK * (g + 1)] for g in range(2)] for t in ub_all]
+        uq = [[t[:, TOK * g : TOK * (g + 1)] for g in range(2)] for t in uq_all]
+        uqs = [[t[:, TOK * g : TOK * (g + 1)] for g in range(2)] for t in uqs_all]
         gl = [keep("gl%d" % g, [P, 4, B], F32) for g in range(2)]
-        gb = [keep("gb%d" % g, [P, 4 * B], BF16) for g in range(2)]
-        gq = [keep("gq%d" % g, [P, B], U32) for g in range(2)]
-        gqs = [keep("gqs%d" % g, [P, B], U8) for g in range(2)]
-        PIECES = ((0, 0, 256), (1, 0, 256), (2, 0, 256), (3, 0, 128), (3, 128, 128))
-        th = {(h, lo): keep("th%d_%d" % (h, lo), [P, 2, n], F32) for h, lo, n in PIECES}
-        sg = {(h, lo): keep("sg%d_%d" % (h, lo), [P, 2, n], F32) for h, lo, n in PIECES}
-        lg = {(h, lo): keep("lg%d_%d" % (h, lo), [P, 2, n], F32) for h, lo, n in PIECES}
-        r = {(h, lo): keep("r%d_%d" % (h, lo), [P, n], F32) for h, lo, n in PIECES}
-        res = {(h, lo): keep("res%d_%d" % (h, lo), [P, 2, n], F32) for h, lo, n in PIECES}
+        gb_all = keep("gb", [P, 2 * 4 * B], BF16)
+        gq_all = keep("gq", [P, 2 * B], U32)
+        gqs_all = keep("gqs", [P, 2 * B], U8)
+        gb = [gb_all[:, 4 * B * g : 4 * B * (g + 1)] for g in range(2)]
+        gq = [gq_all[:, B * g : B * (g + 1)] for g in range(2)]
+        gqs = [gqs_all[:, B * g : B * (g + 1)] for g in range(2)]
+        th = [keep("th%d" % i, [P, 2, 512], F32) for i in range(2)]
+        sg = [keep("sg%d" % i, [P, 2, 512], F32) for i in range(2)]
+        lg = [[keep("lg%d_%d" % (i, a), [P, 512], F32) for a in range(2)] for i in range(2)]
+        res = [[keep("res%d_%d" % (i, a), [P, 512], F32) for a in range(2)] for i in range(2)]
+        r = [keep("r%d" % i, [P, 512], F32) for i in range(2)]
 
         flat = {("u", h, g): keep("flat_u%d_%d" % (h, g), [P, 4, TOK], BF16) for h in range(GROUPS) for g in range(2)}
         flat.update({("g", g): keep("flat_g%d" % g, [P, 4, B], BF16) for g in range(2)})
 
         wide = [keep("wide%d" % g, [P, 4, 2 * TOK], BF16) for g in range(2)]
 
-        gain_col = [keep("gain_col%d" % g, [P, 4], F32) for g in range(2)]
+        gain_col = [keep("gain_col%d" % g, [P, 4], F32) for g in range(4)]
+        hs = {lo: keep("hs%d" % lo, [P, 2, n], F32) for lo, n in HI}
         words_in = {"u": wu_words, "g": wg_words}
         scales_in = {"u": wu_scales, "g": wg_scales}
         held = {}
@@ -230,14 +237,14 @@ def tile_deepinfomaxlocalglobaljsdmap_d1p_kernel(
                     bias=vec[:, 1, g, t : t + 1],
                 )
 
-        def gate(g):
-            nc.vector.tensor_copy(out=gain_col[g][:], in_=vec[:, 2, g, :])
+        def gate(j):
+            nc.vector.tensor_copy(out=gain_col[j][:], in_=vec[:, 2, j // 2, :])
 
-        def g_gain_pool(g):
+        def g_gain_pool(g, a):
             nc.gpsimd.tensor_tensor(
-                out=gb[g][:].rearrange("p (n t) -> p n t", t=4),
-                in0=gl[g][:].rearrange("p t n -> p n t"),
-                in1=gain_col[g][:].unsqueeze(1).to_broadcast([P, B, 4]),
+                out=gb[g][:, 512 * a : 512 * (a + 1)].rearrange("p (n t) -> p n t", t=4),
+                in0=gl[g][:, :, 128 * a : 128 * (a + 1)].rearrange("p t n -> p n t"),
+                in1=gain_col[2 * g + a][:].unsqueeze(1).to_broadcast([P, 128, 4]),
                 op=ALU.mult,
             )
 
@@ -279,70 +286,105 @@ def tile_deepinfomaxlocalglobaljsdmap_d1p_kernel(
             for j in range(n):
                 nc.tensor.matmul(t[:, 0:P], lhsT=ident[:], rhs=ident[:], start=True, stop=True)
 
-        def s_mm(h, k, lo=0, n=TOK):
+        def score_mm(dst, a, h, lo, n):
+            for g in range(2):
+                nc.tensor.matmul_mx(
+                    out=dst,
+                    lhsT=gq[g][:, 128 * a : 128 * (a + 1)].bitcast(FP8X4),
+                    lhsT_scale=gqs[g][:, 128 * a : 128 * (a + 1)],
+                    rhs=uq[h][g][:, lo : lo + n].bitcast(FP8X4),
+                    rhs_scale=uqs[h][g][:, lo : lo + n],
+                    start=(g == 0),
+                    stop=(g == 1),
+                )
+
+        def s_mm_lo(a, k):
             t = bank(k)
-            held["s", h, lo] = t
+            held["lo", a] = t
+            for h in range(2):
+                score_mm(t[:, TOK * h : TOK * (h + 1)], a, h, 0, TOK)
+
+        def s_mm_hi(lo, n, k):
+            t = bank(k)
+            held["hi", lo] = t
             for a in range(2):
-                for g in range(2):
-                    nc.tensor.matmul_mx(
-                        out=t[:, n * a : n * (a + 1)],
-                        lhsT=gq[g][:, 128 * a : 128 * (a + 1)].bitcast(FP8X4),
-                        lhsT_scale=gqs[g][:, 128 * a : 128 * (a + 1)],
-                        rhs=uq[h][g][:, lo : lo + n].bitcast(FP8X4),
-                        rhs_scale=uqs[h][g][:, lo : lo + n],
-                        start=(g == 0),
-                        stop=(g == 1),
-                    )
+                score_mm(t[:, n * a : n * (a + 1)], a, 2 + lo // TOK, lo % TOK, n)
 
-        def s_abs(h, lo=0, n=TOK):
-            src = held["s", h, lo][:, 0 : 2 * n].rearrange("p (a n) -> p a n", a=2)
-            nc.scalar.activation(out=th[h, lo][:], in_=src, func=ACT.Abs, scale=0.5)
+        def hi_bank(lo, n):
+            return held["hi", lo][:, 0 : 2 * n].rearrange("p (a n) -> p a n", a=2)
 
-        def s_tanh(h, lo=0, n=TOK):
-            nc.scalar.activation(out=th[h, lo][:], in_=th[h, lo][:], func=ACT.Tanh)
+        def v_abs(dst, src):
+            nc.vector.scalar_tensor_tensor(out=dst, in0=src, scalar=-1.0, in1=src, op0=ALU.mult, op1=ALU.max)
 
-        def s_tanh_first(h, lo, n):
-            src = held["s", h, lo][:, 0 : 2 * n].rearrange("p (a n) -> p a n", a=2)
-            nc.scalar.activation(out=sg[h, lo][:], in_=src, func=ACT.Tanh, scale=0.5)
+        def abs_first_lo(a):
+            nc.scalar.activation(out=sg[0][:, a, :], in_=held["lo", a][:], func=ACT.Abs, scale=0.5)
 
-        def s_abs_after(h, lo, n):
-            nc.vector.scalar_tensor_tensor(
-                out=th[h, lo][:], in0=sg[h, lo][:], scalar=-1.0, in1=sg[h, lo][:], op0=ALU.mult, op1=ALU.max
-            )
+        def tanh_after_lo(a):
+            nc.scalar.activation(out=th[0][:, a, :], in_=sg[0][:, a, :], func=ACT.Tanh)
 
-        def s_sign(h, lo, n):
-            a = h // 2
-            j0 = 64 * (h % 2) + lo // L
+        def tanh_first_lo(a):
+            nc.scalar.activation(out=sg[0][:, a, :], in_=held["lo", a][:], func=ACT.Tanh, scale=0.5)
+
+        def abs_after_lo(a):
+            v_abs(th[0][:, a, :], sg[0][:, a, :])
+
+        def abs_first_hi(lo, n):
+            nc.scalar.activation(out=hs[lo][:], in_=hi_bank(lo, n), func=ACT.Abs, scale=0.5)
+
+        def tanh_after_hi(lo, n):
+            nc.scalar.activation(out=th[1][:, :, lo : lo + n], in_=hs[lo][:], func=ACT.Tanh)
+
+        def tanh_first_hi(lo, n):
+            nc.scalar.activation(out=hs[lo][:], in_=hi_bank(lo, n), func=ACT.Tanh, scale=0.5)
+
+        def abs_after_hi(lo, n):
+            v_abs(th[1][:, :, lo : lo + n], hs[lo][:])
+
+        def flip(dst, src, j0, n):
             nc.vector.tensor_tensor(
-                out=r[h, lo][:].rearrange("p (j l) -> p j l", l=L),
-                in0=held["s", h, lo][:, n * a : n * (a + 1)].rearrange("p (j l) -> p j l", l=L),
+                out=dst.rearrange("p (j l) -> p j l", l=L),
+                in0=src.rearrange("p (j l) -> p j l", l=L),
                 in1=sign[:, j0 : j0 + n // L].unsqueeze(2).to_broadcast([P, n // L, L]),
                 op=ALU.mult,
             )
 
-        def finish(h, lo, a, src):
-            nc.vector.scalar_tensor_tensor(
-                out=res[h, lo][:, a, :], in0=src, scalar=0.0, in1=lg[h, lo][:, a, :], op0=ALU.max, op1=ALU.subtract
+        def sign_lo():
+            flip(r[0][:], held["lo", 0][:], 0, 512)
+
+        def sign_hi(lo, n):
+            flip(r[1][:, lo : lo + n], held["hi", lo][:, n : 2 * n], lo // L, n)
+
+        def finish(dst, src, log):
+            nc.vector.scalar_tensor_tensor(out=dst, in0=src, scalar=0.0, in1=log, op0=ALU.max, op1=ALU.subtract)
+
+        def finish_diag(i):
+            finish(res[i][i][:], r[i][:], lg[i][i][:])
+
+        def finish_lo():
+            finish(res[0][1][:], held["lo", 1][:], lg[0][1][:])
+
+        def finish_hi(lo, n):
+            finish(res[1][0][:, lo : lo + n], held["hi", lo][:, 0:n], lg[1][0][:, lo : lo + n])
+
+        def s_log(i, a, lo, n):
+            nc.scalar.activation(
+                out=lg[i][a][:, lo : lo + n], in_=th[i][:, a, lo : lo + n], func=ACT.Ln, scale=0.5, bias=half[:]
             )
 
-        def finish_plain(h, lo, n):
-            a = 1 - h // 2
-            finish(h, lo, a, held["s", h, lo][:, n * a : n * (a + 1)])
+        def s_store(i, a, lo, n):
+            nc.sync.dma_start(out=out_rows[:, a, 512 * i + lo : 512 * i + lo + n], in_=res[i][a][:, lo : lo + n])
 
-        def finish_diag(h, lo, n):
-            finish(h, lo, h // 2, r[h, lo][:])
+        def u_quant_both(h):
+            quant(uq_all[h], uqs_all[h], ub_all[h])
+
+        def g_quant_both():
+            quant(gq_all, gqs_all, gb_all)
 
         def make_pick():
             nc.vector.tensor_copy(out=ident_bf[:], in_=ident[:, 0:8])
             nc.vector.tensor_scalar(
                 out=ident_bf[:, 2:4], in0=ident[:, 2:4], scalar1=1.0 / 16.0, scalar2=None, op0=ALU.mult
             )
-
-        def s_log(h, lo=0, n=TOK):
-            nc.scalar.activation(out=lg[h, lo][:], in_=th[h, lo][:], func=ACT.Ln, scale=0.5, bias=half[:])
-
-        def s_store(h, lo, n):
-            nc.sync.dma_start(out=out_rows[:, :, TOK * h + lo : TOK * h + lo + n], in_=res[h, lo][:])
 
         def x_quant(h):
             quant(xq[h], xqs[h], xt[h])
@@ -369,183 +411,178 @@ def tile_deepinfomaxlocalglobaljsdmap_d1p_kernel(
         load_x(xb1, 1, 1)
         load_x(xb0, 0, 1)
         load_vec(2, gain)
-        load_x(xb23, 2, 2)
         load_vec(1, bg)
-        load_y()
         load_vec(0, bu)
-        load_words("u", 0, 512)
-        nc.vector.memset(vec_perm[:], 0.0)
-        nc.vector.memset(half[:], 0.5)
+        load_x(xb23, 2, 2)
+        load_y()
         nc.vector.memset(s_raw["g"][:].bitcast(I32), 0)
         nc.vector.memset(s_raw["u"][:].bitcast(I32), 0)
+        make_pick()
+        nc.vector.memset(vec_perm[:], 0.0)
+        nc.vector.memset(half[:], 0.5)
+        widen(1, 1, 0, "v")
+        widen(1, 0, 1, "v")
+        widen(1, 0, 3, "v")
+        widen(1, 1, 1, "v")
+        widen(1, 1, 2, "v")
+        widen(1, 1, 3, "v")
+        load_words("u", 0, 512)
         load_scales("u")
         load_words("u", 512, 512)
-        nc.scalar.activation(out=warm[:], in_=half[:], func=ACT.Gelu)
-        widen(0, 1, 0, "v")
-        widen(0, 1, 3, "v")
-        make_pick()
-        widen(1, 1, 2, "v")
-        widen(0, 1, 2, "v")
-        widen(1, 1, 1, "v")
-        widen(0, 0, 0, "v")
-        widen(2, 0, 1, "v")
-        widen(2, 1, 3, "v")
-        widen(3, 0, 0, "v")
-        widen(2, 1, 2, "v")
-        widen(3, 1, 1, "v")
-        widen(0, 1, 1, "v")
-        perm_vec()
-        widen(3, 0, 2, "v")
-        widen(2, 0, 3, "v")
-        perm_words("u", 0, nc.vector)
-        widen(1, 1, 0, "s")
-        widen(1, 0, 3, "s")
-        widen(1, 0, 0, "s")
-        widen(1, 0, 1, "s")
-        widen(1, 0, 2, "s")
-        widen(1, 1, 3, "s")
-        widen(2, 1, 0, "s")
-        widen(0, 0, 2, "s")
-        widen(0, 0, 3, "s")
-        widen(2, 0, 2, "s")
-        widen(0, 0, 1, "s")
         warm_pe(0, 1)
         warm_pe(1, 1)
         warm_pe(2, 1)
         warm_pe(3, 1)
-        warm_pe(4, 1)
-        warm_pe(5, 1)
-        turn(1, 6)
-        turn(4, 7)
-        turn_out(1)
-        turn(0, 0)
-        turn_out(4)
-        x_quant(1)
-        perm_scales("u", nc.vector)
-        turn_out(0)
-        vec_mm(1)
-        vec_out()
-        u_mm(1, 0, 0, 2)
-        widen(2, 1, 1, "s")
+        nc.scalar.activation(out=warm[:], in_=half[:], func=ACT.Gelu)
+        widen(1, 0, 2, "s")
+        widen(1, 0, 0, "s")
+        perm_vec()
+        widen(0, 0, 2, "s")
+        widen(0, 1, 1, "s")
+        widen(0, 1, 3, "s")
+        widen(0, 0, 1, "s")
         widen(3, 1, 2, "s")
-        widen(3, 0, 3, "s")
-        u_mm(1, 0, 1, 3)
-        widen(3, 1, 3, "s")
-        widen(3, 0, 1, "s")
+        widen(2, 1, 3, "s")
+        turn(1, 4)
+        vec_mm(5)
+        turn_out(1)
+        warm_pe(6, 1)
+        warm_pe(7, 1)
+        widen(0, 0, 0, "v")
+        widen(0, 1, 0, "v")
+        widen(2, 0, 2, "v")
+        widen(3, 0, 0, "v")
+        widen(2, 0, 0, "v")
+        widen(0, 1, 2, "v")
+        widen(3, 0, 3, "v")
+        vec_out()
+        widen(3, 0, 2, "s")
+        turn(4, 0)
+        widen(2, 0, 1, "s")
+        widen(2, 1, 0, "v")
+        widen(0, 0, 3, "v")
+        turn(0, 1)
+        widen(3, 0, 1, "v")
+        x_quant(1)
+        widen(3, 1, 3, "v")
+        perm_words("u", 0, nc.vector)
+        perm_scales("u", nc.vector)
         widen(3, 1, 0, "s")
-        widen(2, 0, 0, "s")
-        x_quant(4)
+        widen(3, 1, 1, "s")
+        turn_out(4)
+        turn(3, 2)
+        widen(2, 1, 1, "s")
+        widen(2, 0, 3, "s")
+        turn_out(0)
+        turn_out(3)
+        u_mm(1, 0, 1, 3)
+        gate(0)
+        widen(2, 1, 2, "v")
         perm_words("u", 1, nc.vector)
-        x_quant(0)
         load_words("g", 0, E)
         load_scales("g")
-        u_mm_pair(1, 1, 0, 4)
-        turn(3, 5)
-        u_out(1, 0, 0)
-        u_bias(1, 1, 0)
+        x_quant(4)
         u_out(1, 0, 1)
-        perm_words("g", 0, nc.vector)
-        u_mm(0, 0, 0, 6)
-        perm_scales("g", nc.vector)
-        perm_words("g", 1, nc.vector)
-        u_quant(1, 0)
+        u_mm(1, 0, 0, 4)
+        u_mm_pair(1, 1, 0, 6)
+        u_bias(1, 1, 0)
         u_mm_pair(1, 1, 1, 7)
-        g_mm(0, 0, 0)
-        turn_out(3)
-        g_mm(1, 1, 1)
+        turn(2, 5)
+        x_quant(0)
+        perm_words("g", 0, nc.vector)
+        perm_words("g", 1, nc.vector)
+        perm_scales("g", nc.vector)
+        u_mm(0, 1, 1, 0)
+        u_out(1, 0, 0)
+        g_mm(0, 0, 1)
         g_mm(0, 1, 2)
-        u_out(0, 0, 0)
-        u_mm(0, 1, 1, 4)
         x_quant(3)
-        g_mm(1, 0, 3)
+        u_mm_pair(0, 0, 0, 3)
         u_bias(1, 1, 1)
-        u_weave(1, 1)
-        u_out(0, 1, 1)
-        u_mm(0, 1, 0, 5)
-        u_mm(0, 0, 1, 6)
-        turn(2, 7)
-        u_out(0, 0, 1)
-        u_mm(3, 1, 1, 4)
-        u_out(0, 1, 0)
-        gelu(1, 1)
-        gelu(0, 1)
-        gelu(0, 0)
-        u_mm(3, 0, 0, 6)
-        warm_pe(5, 1)
-        u_quant(1, 1)
-        u_quant(0, 1)
-        u_out(3, 1, 1)
         turn_out(2)
+        gelu(0, 0)
+        gelu(0, 1)
+        g_mm(1, 0, 6)
+        u_mm(0, 1, 0, 4)
+        u_mm(3, 0, 1, 7)
         gelu(1, 0)
+        g_mm(1, 1, 5)
+        gelu(1, 1)
+        u_weave(1, 1)
         x_quant(2)
-        g_scale(0, 1)
-        g_scale(0, 0)
-        u_quant(3, 1, 128, 128)
-        u_quant(0, 0)
-        g_scale(1, 1)
+        u_quant_both(1)
         g_scale(1, 0)
-        g_weave(0)
-        u_out(3, 0, 0)
-        g_weave(1)
-        g_quant(0)
-        g_quant(1)
-        u_mm(3, 0, 1, 1)
+        g_scale(1, 1)
+        u_mm(3, 0, 0, 1)
+        u_mm(3, 1, 0, 2)
         u_out(3, 0, 1)
-        u_mm_pair(2, 0, 1, 2)
-        u_mm_pair(2, 0, 0, 0)
-        u_bias(2, 0, 1)
-        u_mm_pair(2, 1, 1, 5)
+        u_mm_pair(2, 1, 1, 6)
+        u_out(0, 1, 1)
+        gate(1)
+        u_out(0, 1, 0)
+        u_mm(3, 1, 1, 5)
+        u_mm_pair(0, 0, 1, 7)
+        u_bias(0, 0, 1)
+        u_bias(0, 0, 0)
+        u_out(3, 0, 0)
+        u_out(3, 1, 1)
+        u_mm_pair(2, 0, 1, 0)
+        u_mm_pair(2, 0, 0, 4)
         u_bias(2, 0, 0)
-        u_mm_pair(2, 1, 0, 4)
-        warm_pe(7, 1)
-        u_weave(2, 0)
+        u_bias(2, 0, 1)
         u_bias(2, 1, 1)
+        u_mm_pair(2, 1, 0, 7)
+        warm_pe(3, 1)
+        warm_pe(1, 1)
         u_bias(2, 1, 0)
-        u_mm(3, 1, 0, 3)
+        g_gain_pool(0, 0)
+        g_gain_pool(0, 1)
+        g_weave(1)
+        u_weave(0, 0)
+        g_quant(0)
+        u_quant_both(0)
+        g_quant(1)
+        u_weave(2, 0)
         u_weave(2, 1)
         u_quant(2, 0)
         u_quant(2, 1)
-        s_mm(1, 6, 0, 256)
-        s_abs(1, 0, 256)
-        s_mm(0, 1, 0, 256)
-        s_mm(2, 2, 0, 256)
+        u_quant(3, 1, 128, 128)
+        s_mm_lo(0, 5)
+        s_mm_lo(1, 4)
+        abs_first_lo(0)
+        s_mm_hi(0, 256, 0)
         u_out(3, 1, 0)
         u_quant(3, 0, 128, 128)
-        s_mm(3, 0, 128, 128)
-        s_abs(0, 0, 256)
-        s_tanh(1, 0, 256)
-        s_tanh(0, 0, 256)
         u_quant(3, 0, 0, 128)
         u_quant(3, 1, 0, 128)
-        s_tanh_first(2, 0, 256)
-        s_tanh_first(3, 128, 128)
-        s_sign(1, 0, 256)
-        s_mm(3, 7, 0, 128)
-        s_sign(0, 0, 256)
-        s_tanh_first(3, 0, 128)
-        s_abs_after(2, 0, 256)
-        s_abs_after(3, 128, 128)
-        s_abs_after(3, 0, 128)
-        s_sign(3, 128, 128)
-        s_log(3, 0, 128)
-        s_sign(3, 0, 128)
-        s_sign(2, 0, 256)
-        finish_plain(3, 0, 128)
-        finish_diag(3, 0, 128)
-        s_log(3, 128, 128)
-        finish_diag(3, 128, 128)
-        finish_plain(3, 128, 128)
-        s_log(0, 0, 256)
-        finish_diag(0, 0, 256)
-        finish_plain(0, 0, 256)
-        s_log(1, 0, 256)
-        s_log(2, 0, 256)
-        finish_plain(1, 0, 256)
-        finish_diag(1, 0, 256)
-        finish_plain(2, 0, 256)
-        finish_diag(2, 0, 256)
-        s_store(3, 0, 128)
-        s_store(3, 128, 128)
-        s_store(0, 0, 256)
-        s_store(1, 0, 256)
-        s_store(2, 0, 256)
+        abs_first_lo(1)
+        tanh_after_lo(0)
+        tanh_after_lo(1)
+        s_mm_hi(384, 128, 6)
+        tanh_first_hi(0, 256)
+        s_mm_hi(256, 128, 3)
+        tanh_first_hi(384, 128)
+        tanh_first_hi(256, 128)
+        s_log(0, 0, 0, 512)
+        sign_lo()
+        sign_hi(0, 256)
+        abs_after_hi(384, 128)
+        sign_hi(256, 128)
+        sign_hi(384, 128)
+        abs_after_hi(256, 128)
+        abs_after_hi(0, 256)
+        finish_diag(0)
+        s_log(0, 1, 0, 512)
+        s_log(1, 1, 0, 512)
+        s_log(1, 0, 0, 256)
+        s_log(1, 0, 256, 256)
+        finish_lo()
+        finish_diag(1)
+        finish_hi(0, 256)
+        finish_hi(256, 128)
+        finish_hi(384, 128)
+        s_store(0, 0, 0, 512)
+        s_store(0, 1, 0, 512)
+        s_store(1, 1, 0, 512)
+        s_store(1, 0, 0, 256)
+        s_store(1, 0, 256, 256)

from contextlib import ExitStack

import concourse.mybir as mybir
from concourse.masks import make_identity

F32 = mybir.dt.float32
BF16 = mybir.dt.bfloat16
I32 = mybir.dt.int32
U32 = mybir.dt.uint32
U8 = mybir.dt.uint8
FP8 = mybir.dt.float8_e4m3fn
FP8X4 = mybir.dt.float8_e4m3fn_x4
ACT = mybir.ActivationFunctionType
ALU = mybir.AluOpType

B, L, D, E = 256, 4, 512, 1024
P = 128
GROUPS = 4
TOK = 256
HI = ((0, 256), (256, 128), (384, 128))
FLOPS = 2 * (B * L * D * E + B * D * E + B * E * B * L)


def tile_deepinfomaxlocalglobaljsdmap_d1p_kernel(
    tc, x_bytes, x_scale, y, wu_words, wu_scales, bu, wg_words, wg_scales, bg, gain, out
):
    nc = tc.nc
    with ExitStack() as ctx:
        sb = ctx.enter_context(tc.tile_pool(name="sb", bufs=1))
        ps = ctx.enter_context(tc.psum_pool(name="ps", bufs=1))
        ctx.enter_context(tc.manual_schedule())

        def keep(name, shape, dtype):
            return sb.tile(shape, dtype, name=name, align_bytes=64)

        def bank(k):
            return ps.tile([P, 512], F32, name="bank%d" % k)

        x_rows = x_bytes.rearrange("b l k -> (b l) k").rearrange("(h p c) k -> p h (c k)", p=P, c=2)
        xs_rows = x_scale.rearrange("b l q -> (b l) q").rearrange("(h p c) q -> p h (c q)", p=P, c=2)
        out_rows = out.rearrange("(a p) j l -> p a (j l)", p=P)

        xs = keep("xs", [P, GROUPS, 8], F32)
        xb0 = keep("xb0", [P, 1, 2 * D], U8)
        xb1 = keep("xb1", [P, 1, 2 * D], U8)
        xb23 = keep("xb23", [P, 2, 2 * D], U8)
        xb = [xb0[:, 0, :], xb1[:, 0, :], xb23[:, 0, :], xb23[:, 1, :]]
        xw = [[keep("xw%d_%d" % (h, c), [P, D], BF16) for c in range(2)] for h in range(GROUPS)]
        yb = keep("yb", [P, 2, D], BF16)
        xt = [keep("xt%d" % h, [P, 4 * TOK], BF16) for h in range(GROUPS + 1)]
        xq_all = keep("xq_all", [P, (GROUPS + 1) * TOK], U32)
        xqs_all = keep("xqs_all", [P, (GROUPS + 1) * TOK], U8)
        xq = [xq_all[:, TOK * h : TOK * (h + 1)] for h in range(GROUPS + 1)]
        xqs = [xqs_all[:, TOK * h : TOK * (h + 1)] for h in range(GROUPS + 1)]
        w_raw = {w: keep("wraw_%s" % w, [P, E], U32) for w in "ug"}
        w_perm = {(w, g): keep("wperm_%s%d" % (w, g), [P, 512], U32) for w in "ug" for g in range(2)}
        s_raw = {w: keep("sraw_%s" % w, [P, E], U8) for w in "ug"}
        s_perm = {w: keep("sperm_%s" % w, [P, E], U8) for w in "ug"}
        vec_rows = keep("vec_rows", [4, E], BF16)
        vec_perm = keep("vec_perm", [P, E], BF16)
        vec = keep("vec", [P, 3, 2, 4], F32)
        ident = keep("ident", [P, P], F32)
        ident_bf = keep("ident_bf", [P, 8], BF16)
        half = keep("half", [P, 1], F32)
        warm = keep("warm", [P, 1], F32)
        sign = keep("sign", [P, P], F32)
        ub_all = [keep("ub%d" % h, [P, 2 * 4 * TOK], BF16) for h in range(GROUPS)]
        uq_all = [keep("uq%d" % h, [P, 2 * TOK], U32) for h in range(GROUPS)]
        uqs_all = [keep("uqs%d" % h, [P, 2 * TOK], U8) for h in range(GROUPS)]
        ub = [[t[:, 4 * TOK * g : 4 * TOK * (g + 1)] for g in range(2)] for t in ub_all]
        uq = [[t[:, TOK * g : TOK * (g + 1)] for g in range(2)] for t in uq_all]
        uqs = [[t[:, TOK * g : TOK * (g + 1)] for g in range(2)] for t in uqs_all]
        gl = [keep("gl%d" % g, [P, 4, B], F32) for g in range(2)]
        gb_all = keep("gb", [P, 2 * 4 * B], BF16)
        gq_all = keep("gq", [P, 2 * B], U32)
        gqs_all = keep("gqs", [P, 2 * B], U8)
        gb = [gb_all[:, 4 * B * g : 4 * B * (g + 1)] for g in range(2)]
        gq = [gq_all[:, B * g : B * (g + 1)] for g in range(2)]
        gqs = [gqs_all[:, B * g : B * (g + 1)] for g in range(2)]
        th = [keep("th%d" % i, [P, 2, 512], F32) for i in range(2)]
        sg = [keep("sg%d" % i, [P, 2, 512], F32) for i in range(2)]
        lg = [[keep("lg%d_%d" % (i, a), [P, 512], F32) for a in range(2)] for i in range(2)]
        res = [[keep("res%d_%d" % (i, a), [P, 512], F32) for a in range(2)] for i in range(2)]
        r = [keep("r%d" % i, [P, 512], F32) for i in range(2)]

        flat = {("u", h, g): keep("flat_u%d_%d" % (h, g), [P, 4, TOK], BF16) for h in range(GROUPS) for g in range(2)}
        flat.update({("g", g): keep("flat_g%d" % g, [P, 4, B], BF16) for g in range(2)})

        wide = [keep("wide%d" % g, [P, 4, 2 * TOK], BF16) for g in range(2)]

        gain_col = [keep("gain_col%d" % g, [P, 4], F32) for g in range(4)]
        hs = {lo: keep("hs%d" % lo, [P, 2, n], F32) for lo, n in HI}
        words_in = {"u": wu_words, "g": wg_words}
        scales_in = {"u": wu_scales, "g": wg_scales}
        held = {}

        def load_scales(w):
            for q in range(4):
                nc.sync.dma_start(
                    out=s_raw[w][32 * q : 32 * q + 4, :].bitcast(I32),
                    in_=scales_in[w][0, 4 * q : 4 * q + 4, :].bitcast(I32),
                )

        def words(w):
            return words_in[w][0].rearrange("p n t -> p (n t)").bitcast(I32)

        def widen(h, c, q, eng):
            src = xb[h][:, c * D + 128 * q : c * D + 128 * (q + 1)].bitcast(FP8)
            dst = xw[h][c][:, 128 * q : 128 * (q + 1)]
            col = xs[:, h, 4 * c + q : 4 * c + q + 1]
            if eng == "v":
                nc.vector.tensor_scalar(out=dst, in0=src, scalar1=col, scalar2=None, op0=ALU.mult)
            else:
                nc.scalar.activation(out=dst, in_=src, func=ACT.Copy, scale=col)

        def turn(h, k):
            rows = [xw[h][c][:] for c in range(2)] if h < GROUPS else [yb[:, c, :] for c in range(2)]
            t = bank(k)
            held["t", h] = t
            for c in range(2):
                w32 = rows[c].bitcast(F32)
                for u in range(2):
                    j = 2 * c + u
                    nc.tensor.transpose(t[:, 128 * j : 128 * (j + 1)], w32[:, u:256:2], ident[:])

        def turn_out(h):
            nc.scalar.copy(
                out=xt[h][:].bitcast(F32).rearrange("k (m i j) -> k m j i", i=2, j=4),
                in_=held["t", h][:].rearrange("k (j m i) -> k m j i", i=2, j=4),
            )

        def quant(codes, scales, src):
            nc.vector.quantize_mx(out=codes[:].bitcast(FP8X4), scales=scales[:], in_=src[:])

        def perm_words(w, g, eng):
            src = w_raw[w][:, 512 * g : 512 * (g + 1)]
            eng.tensor_copy(
                out=w_perm[w, g][:].bitcast(I32).rearrange("p (t q r) -> p t q r", t=4, r=8),
                in_=src.bitcast(I32).rearrange("p (q t r) -> p t q r", t=4, r=8),
            )

        def perm_scales(w, eng):
            eng.tensor_copy(
                out=s_perm[w][:].bitcast(I32).rearrange("p (t m r) -> p t m r", t=4, r=2),
                in_=s_raw[w][:].bitcast(I32).rearrange("p (m t r) -> p t m r", t=4, r=2),
            )

        def first_mm(dst, w, g, t, h, cols):
            nc.tensor.matmul_mx(
                out=dst,
                lhsT=w_perm[w, g][:, 128 * t : 128 * (t + 1)].bitcast(FP8X4),
                lhsT_scale=s_perm[w][:, 256 * t + 128 * g : 256 * t + 128 * (g + 1)],
                rhs=xq_all[:, TOK * h + cols.start : TOK * h + cols.stop].bitcast(FP8X4),
                rhs_scale=xqs_all[:, TOK * h + cols.start : TOK * h + cols.stop],
                start=True,
                stop=True,
            )

        def u_mm(h, g, a, k):
            t = bank(k)
            held["u", h, g, a] = t
            for j in range(4):
                first_mm(t[:, 128 * j : 128 * (j + 1)], "u", g, j, h, slice(128 * a, 128 * (a + 1)))

        def u_out(h, g, a):
            nc.vector.tensor_tensor(
                out=ub[h][g][:, 512 * a : 512 * (a + 1)].rearrange("p (m i t) -> p m t i", i=2, t=4),
                in0=held["u", h, g, a][:].rearrange("p (t m i) -> p m t i", i=2, t=4),
                in1=vec[:, 0, g, :].unsqueeze(1).unsqueeze(3).to_broadcast([P, 64, 4, 2]),
                op=ALU.add,
            )

        def u_quant(h, g, lo=0, n=TOK):
            quant(uq[h][g][:, lo : lo + n], uqs[h][g][:, lo : lo + n], ub[h][g][:, 4 * lo : 4 * (lo + n)])

        def u_mm_pair(h, g, a, k):
            t = bank(k)
            held["u", h, g, a] = t
            for j in range(2):
                first_mm(t[:, 256 * j : 256 * (j + 1)], "u", g, 2 * a + j, h, slice(0, TOK))

        def u_bias(h, g, a):
            for j in range(2):
                t = 2 * a + j
                nc.scalar.activation(
                    out=flat["u", h, g][:, t, :],
                    in_=held["u", h, g, a][:, 256 * j : 256 * (j + 1)],
                    func=ACT.Identity,
                    bias=vec[:, 0, g, t : t + 1],
                )

        def u_mm_wide(g, t, k):
            b = bank(k)
            held["w", g, t] = b
            first_mm(b[:], "u", g, t, 1, slice(0, 2 * TOK))

        def u_bias_wide(g, t):
            nc.scalar.activation(
                out=wide[g][:, t, :], in_=held["w", g, t][:], func=ACT.Identity, bias=vec[:, 0, g, t : t + 1]
            )

        def u_weave_wide(h, g, eng):
            weave(ub[h][g], wide[g][:, :, TOK * (h - 1) : TOK * h], eng)

        def weave(dst, src, eng=nc.vector):
            eng.tensor_copy(
                out=dst[:].rearrange("p (m i t) -> p m t i", i=4, t=4),
                in_=src[:].rearrange("p t (m i) -> p m t i", i=4),
            )

        def u_weave(h, g):
            weave(ub[h][g], flat["u", h, g])

        def g_scale(g, a):
            for j in range(2):
                t = 2 * a + j
                nc.scalar.activation(
                    out=flat["g", g][:, t, :], in_=gl[g][:, t, :], func=ACT.Copy, scale=vec[:, 2, g, t : t + 1]
                )

        def g_weave(g):
            weave(gb[g], flat["g", g])

        def g_mm(g, a, k):
            t = bank(k)
            held["g", g, a] = t
            for j in range(2):
                first_mm(t[:, 256 * j : 256 * (j + 1)], "g", g, 2 * a + j, GROUPS, slice(0, B))

        def gelu(g, a):
            for j in range(2):
                t = 2 * a + j
                nc.scalar.activation(
                    out=gl[g][:, t, :],
                    in_=held["g", g, a][:, 256 * j : 256 * (j + 1)],
                    func=ACT.Gelu,
                    bias=vec[:, 1, g, t : t + 1],
                )

        def gate(j):
            nc.vector.tensor_copy(out=gain_col[j][:], in_=vec[:, 2, j // 2, :])

        def g_gain_pool(g, a):
            nc.gpsimd.tensor_tensor(
                out=gb[g][:, 512 * a : 512 * (a + 1)].rearrange("p (n t) -> p n t", t=4),
                in0=gl[g][:, :, 128 * a : 128 * (a + 1)].rearrange("p t n -> p n t"),
                in1=gain_col[2 * g + a][:].unsqueeze(1).to_broadcast([P, 128, 4]),
                op=ALU.mult,
            )

        def g_gain(g, eng):
            eng.tensor_tensor(
                out=gb[g][:].rearrange("p (m i t) -> p m t i", i=2, t=4),
                in0=gl[g][:].rearrange("p t (m i) -> p m t i", i=2),
                in1=vec[:, 2, g, :].unsqueeze(1).unsqueeze(3).to_broadcast([P, B // 2, 4, 2]),
                op=ALU.mult,
            )

        def load_words(w, lo, n):
            nc.sync.dma_start(out=w_raw[w][:, lo : lo + n].bitcast(I32), in_=words(w)[:, lo : lo + n])

        def load_vec(v, src):
            nc.sync.dma_start(out=vec_rows[v : v + 1, :], in_=src.unsqueeze(0))

        def perm_vec():
            nc.vector.tensor_copy(
                out=vec_perm[0:3, :].rearrange("p (t m r) -> p t m r", t=4, r=8),
                in_=vec_rows[0:3, :].rearrange("p (m t r) -> p t m r", t=4, r=8),
            )

        def vec_mm(k):
            t = bank(k)
            held["v"] = t
            for j in range(8):
                nc.tensor.matmul(
                    t[:, 4 * j : 4 * (j + 1)], lhsT=vec_perm[:, 128 * j : 128 * (j + 1)], rhs=ident_bf[:, 0:4],
                    start=True, stop=True,
                )

        def vec_out():
            for g in range(1):
                nc.scalar.copy(out=vec[:], in_=held["v"][:, 0:32].rearrange("p (t g v) -> p v g t", t=4, g=2)[:, 0:3])

        def warm_pe(k, n):
            t = bank(k)
            for j in range(n):
                nc.tensor.matmul(t[:, 0:P], lhsT=ident[:], rhs=ident[:], start=True, stop=True)

        def score_mm(dst, a, h, lo, n):
            for g in range(2):
                nc.tensor.matmul_mx(
                    out=dst,
                    lhsT=gq[g][:, 128 * a : 128 * (a + 1)].bitcast(FP8X4),
                    lhsT_scale=gqs[g][:, 128 * a : 128 * (a + 1)],
                    rhs=uq[h][g][:, lo : lo + n].bitcast(FP8X4),
                    rhs_scale=uqs[h][g][:, lo : lo + n],
                    start=(g == 0),
                    stop=(g == 1),
                )

        def s_mm_lo(a, k):
            t = bank(k)
            held["lo", a] = t
            for h in range(2):
                score_mm(t[:, TOK * h : TOK * (h + 1)], a, h, 0, TOK)

        def s_mm_hi(lo, n, k):
            t = bank(k)
            held["hi", lo] = t
            for a in range(2):
                score_mm(t[:, n * a : n * (a + 1)], a, 2 + lo // TOK, lo % TOK, n)

        def hi_bank(lo, n):
            return held["hi", lo][:, 0 : 2 * n].rearrange("p (a n) -> p a n", a=2)

        def v_abs(dst, src):
            nc.vector.scalar_tensor_tensor(out=dst, in0=src, scalar=-1.0, in1=src, op0=ALU.mult, op1=ALU.max)

        def abs_first_lo(a):
            nc.scalar.activation(out=sg[0][:, a, :], in_=held["lo", a][:], func=ACT.Abs, scale=0.5)

        def tanh_after_lo(a):
            nc.scalar.activation(out=th[0][:, a, :], in_=sg[0][:, a, :], func=ACT.Tanh)

        def tanh_first_lo(a):
            nc.scalar.activation(out=sg[0][:, a, :], in_=held["lo", a][:], func=ACT.Tanh, scale=0.5)

        def abs_after_lo(a):
            v_abs(th[0][:, a, :], sg[0][:, a, :])

        def abs_first_hi(lo, n):
            nc.scalar.activation(out=hs[lo][:], in_=hi_bank(lo, n), func=ACT.Abs, scale=0.5)

        def tanh_after_hi(lo, n):
            nc.scalar.activation(out=th[1][:, :, lo : lo + n], in_=hs[lo][:], func=ACT.Tanh)

        def tanh_first_hi(lo, n):
            nc.scalar.activation(out=hs[lo][:], in_=hi_bank(lo, n), func=ACT.Tanh, scale=0.5)

        def abs_after_hi(lo, n):
            v_abs(th[1][:, :, lo : lo + n], hs[lo][:])

        def flip(dst, src, j0, n):
            nc.vector.tensor_tensor(
                out=dst.rearrange("p (j l) -> p j l", l=L),
                in0=src.rearrange("p (j l) -> p j l", l=L),
                in1=sign[:, j0 : j0 + n // L].unsqueeze(2).to_broadcast([P, n // L, L]),
                op=ALU.mult,
            )

        def sign_lo():
            flip(r[0][:], held["lo", 0][:], 0, 512)

        def sign_hi(lo, n):
            flip(r[1][:, lo : lo + n], held["hi", lo][:, n : 2 * n], lo // L, n)

        def finish(dst, src, log):
            nc.vector.scalar_tensor_tensor(out=dst, in0=src, scalar=0.0, in1=log, op0=ALU.max, op1=ALU.subtract)

        def finish_diag(i):
            finish(res[i][i][:], r[i][:], lg[i][i][:])

        def finish_lo():
            finish(res[0][1][:], held["lo", 1][:], lg[0][1][:])

        def finish_hi(lo, n):
            finish(res[1][0][:, lo : lo + n], held["hi", lo][:, 0:n], lg[1][0][:, lo : lo + n])

        def s_log(i, a, lo, n):
            nc.scalar.activation(
                out=lg[i][a][:, lo : lo + n], in_=th[i][:, a, lo : lo + n], func=ACT.Ln, scale=0.5, bias=half[:]
            )

        def s_store(i, a, lo, n):
            nc.sync.dma_start(out=out_rows[:, a, 512 * i + lo : 512 * i + lo + n], in_=res[i][a][:, lo : lo + n])

        def u_quant_both(h):
            quant(uq_all[h], uqs_all[h], ub_all[h])

        def g_quant_both():
            quant(gq_all, gqs_all, gb_all)

        def make_pick():
            nc.vector.tensor_copy(out=ident_bf[:], in_=ident[:, 0:8])
            nc.vector.tensor_scalar(
                out=ident_bf[:, 2:4], in0=ident[:, 2:4], scalar1=1.0 / 16.0, scalar2=None, op0=ALU.mult
            )

        def x_quant(h):
            quant(xq[h], xqs[h], xt[h])

        def g_quant(g):
            quant(gq[g], gqs[g], gb[g])

        def make_sign():
            nc.gpsimd.memset(sign[:], 1.0)
            nc.gpsimd.affine_select(
                out=sign[:], in_=sign[:], pattern=[[-1, P]], compare_op=ALU.not_equal, fill=-1.0, base=0,
                channel_multiplier=1,
            )

        def load_x(tile, lo, n):
            nc.sync.dma_start(out=tile[:], in_=x_rows[:, lo : lo + n, :])

        def load_y():
            nc.sync.dma_start(out=yb[:].rearrange("p c k -> p (c k)"), in_=y.rearrange("(p c) k -> p (c k)", c=2))

        make_identity(nc, ident[:])
        make_sign()
        nc.sync.dma_start(out=xs[:], in_=xs_rows)
        load_x(xb1, 1, 1)
        load_x(xb0, 0, 1)
        load_vec(2, gain)
        load_vec(1, bg)
        load_vec(0, bu)
        load_x(xb23, 2, 2)
        load_y()
        nc.vector.memset(s_raw["g"][:].bitcast(I32), 0)
        nc.vector.memset(s_raw["u"][:].bitcast(I32), 0)
        make_pick()
        nc.vector.memset(vec_perm[:], 0.0)
        nc.vector.memset(half[:], 0.5)
        widen(1, 1, 0, "v")
        widen(1, 0, 1, "v")
        widen(1, 0, 3, "v")
        widen(1, 1, 1, "v")
        widen(1, 1, 2, "v")
        widen(1, 1, 3, "v")
        load_words("u", 0, 512)
        load_scales("u")
        load_words("u", 512, 512)
        warm_pe(0, 1)
        warm_pe(1, 1)
        warm_pe(2, 1)
        warm_pe(3, 1)
        nc.scalar.activation(out=warm[:], in_=half[:], func=ACT.Gelu)
        widen(1, 0, 2, "s")
        widen(1, 0, 0, "s")
        perm_vec()
        widen(0, 0, 2, "s")
        widen(0, 1, 1, "s")
        widen(0, 1, 3, "s")
        widen(0, 0, 1, "s")
        widen(3, 1, 2, "s")
        widen(2, 1, 3, "s")
        turn(1, 4)
        vec_mm(5)
        turn_out(1)
        warm_pe(6, 1)
        warm_pe(7, 1)
        widen(0, 0, 0, "v")
        widen(0, 1, 0, "v")
        widen(2, 0, 2, "v")
        widen(3, 0, 0, "v")
        widen(2, 0, 0, "v")
        widen(0, 1, 2, "v")
        widen(3, 0, 3, "v")
        vec_out()
        widen(3, 0, 2, "s")
        turn(4, 0)
        widen(2, 0, 1, "s")
        widen(2, 1, 0, "v")
        widen(0, 0, 3, "v")
        turn(0, 1)
        widen(3, 0, 1, "v")
        x_quant(1)
        widen(3, 1, 3, "v")
        perm_words("u", 0, nc.vector)
        perm_scales("u", nc.vector)
        widen(3, 1, 0, "s")
        widen(3, 1, 1, "s")
        turn_out(4)
        turn(3, 2)
        widen(2, 1, 1, "s")
        widen(2, 0, 3, "s")
        turn_out(0)
        turn_out(3)
        u_mm(1, 0, 1, 3)
        gate(0)
        widen(2, 1, 2, "v")
        perm_words("u", 1, nc.vector)
        load_words("g", 0, E)
        load_scales("g")
        x_quant(4)
        u_out(1, 0, 1)
        u_mm(1, 0, 0, 4)
        u_mm_pair(1, 1, 0, 6)
        u_bias(1, 1, 0)
        u_mm_pair(1, 1, 1, 7)
        turn(2, 5)
        x_quant(0)
        perm_words("g", 0, nc.vector)
        perm_words("g", 1, nc.vector)
        perm_scales("g", nc.vector)
        u_mm(0, 1, 1, 0)
        u_out(1, 0, 0)
        g_mm(0, 0, 1)
        g_mm(0, 1, 2)
        x_quant(3)
        u_mm_pair(0, 0, 0, 3)
        u_bias(1, 1, 1)
        turn_out(2)
        gelu(0, 0)
        gelu(0, 1)
        g_mm(1, 0, 6)
        u_mm(0, 1, 0, 4)
        u_mm(3, 0, 1, 7)
        gelu(1, 0)
        g_mm(1, 1, 5)
        gelu(1, 1)
        u_weave(1, 1)
        x_quant(2)
        u_quant_both(1)
        g_scale(1, 0)
        g_scale(1, 1)
        u_mm(3, 0, 0, 1)
        u_mm(3, 1, 0, 2)
        u_out(3, 0, 1)
        u_mm_pair(2, 1, 1, 6)
        u_out(0, 1, 1)
        gate(1)
        u_out(0, 1, 0)
        u_mm(3, 1, 1, 5)
        u_mm_pair(0, 0, 1, 7)
        u_bias(0, 0, 1)
        u_bias(0, 0, 0)
        u_out(3, 0, 0)
        u_out(3, 1, 1)
        u_mm_pair(2, 0, 1, 0)
        u_mm_pair(2, 0, 0, 4)
        u_bias(2, 0, 0)
        u_bias(2, 0, 1)
        u_bias(2, 1, 1)
        u_mm_pair(2, 1, 0, 7)
        warm_pe(3, 1)
        warm_pe(1, 1)
        u_bias(2, 1, 0)
        g_gain_pool(0, 0)
        g_gain_pool(0, 1)
        g_weave(1)
        u_weave(0, 0)
        g_quant(0)
        u_quant_both(0)
        g_quant(1)
        u_weave(2, 0)
        u_weave(2, 1)
        u_quant(2, 0)
        u_quant(2, 1)
        u_quant(3, 1, 128, 128)
        s_mm_lo(0, 5)
        s_mm_lo(1, 4)
        abs_first_lo(0)
        s_mm_hi(0, 256, 0)
        u_out(3, 1, 0)
        u_quant(3, 0, 128, 128)
        u_quant(3, 0, 0, 128)
        u_quant(3, 1, 0, 128)
        abs_first_lo(1)
        tanh_after_lo(0)
        tanh_after_lo(1)
        s_mm_hi(384, 128, 6)
        tanh_first_hi(0, 256)
        s_mm_hi(256, 128, 3)
        tanh_first_hi(384, 128)
        tanh_first_hi(256, 128)
        s_log(0, 0, 0, 512)
        sign_lo()
        sign_hi(0, 256)
        abs_after_hi(384, 128)
        sign_hi(256, 128)
        sign_hi(384, 128)
        abs_after_hi(256, 128)
        abs_after_hi(0, 256)
        finish_diag(0)
        s_log(0, 1, 0, 512)
        s_log(1, 1, 0, 512)
        s_log(1, 0, 0, 256)
        s_log(1, 0, 256, 256)
        finish_lo()
        finish_diag(1)
        finish_hi(0, 256)
        finish_hi(256, 128)
        finish_hi(384, 128)
        s_store(0, 0, 0, 512)
        s_store(0, 1, 0, 512)
        s_store(1, 1, 0, 512)
        s_store(1, 0, 0, 256)
        s_store(1, 0, 256, 256)
